import numpy as np
import ml_dtypes


def mxq(x, axis, fmt="e4m3"):
    dtype, down = {"e4m3": (ml_dtypes.float8_e4m3fn, 7), "e5m2": (ml_dtypes.float8_e5m2, 14)}[fmt]
    v = np.moveaxis(np.asarray(x, np.float32).astype(ml_dtypes.bfloat16).astype(np.float64), axis, -1)
    blocks = v.reshape(v.shape[:-1] + (-1, 32))
    amax = np.abs(blocks).max(-1, keepdims=True)
    byte = np.maximum(np.where(amax > 0, np.frexp(amax)[1] - 1 + 127, 0) - down, 1)
    scale = np.exp2(byte - 127.0)
    codes = (blocks / scale).astype(np.float32).astype(dtype).astype(np.float64)
    return np.moveaxis((codes * scale).reshape(v.shape), -1, axis)


WIDE = False


def mx_kscale(k):
    if not WIDE:
        return np.ones(k)
    levels = np.array([10, -10, 5, -5, 0])
    if k % 512:
        return np.exp2(np.random.permutation(np.resize(levels, k // 32))).repeat(32)
    a = np.empty((k // 512, 16))
    for p in range(k // 512):
        a[p, :8] = np.random.permutation(np.resize(levels, 8))
        for g in range(8):
            far = levels[np.abs(levels - a[p, g]) >= 10]
            a[p, g + 8] = far[np.random.randint(len(far))]
    return np.exp2(a.ravel()).repeat(32)


BF16 = ml_dtypes.bfloat16


def bf(x):
    return np.asarray(x, np.float32).astype(BF16)


def f64(x):
    return np.asarray(x).astype(np.float64)

def planes(Y):
    n, m = Y.shape
    b = f64(bf(Y)).reshape(n // 32, 32, m)
    amax = np.abs(b).max(1)
    byte = np.clip(np.where(amax > 0, np.frexp(amax)[1] - 1 + 127 - 7, 1), 1, 254)
    codes = (b * np.exp2(127.0 - byte)[:, None, :]).reshape(n, m).astype(np.float32).astype(ml_dtypes.float8_e4m3fn).view(np.uint8)
    words = codes.reshape(n // 512, 128, 4, m).transpose(0, 1, 3, 2)
    return np.ascontiguousarray(words), np.ascontiguousarray(byte.astype(np.uint8).reshape(n // 512, 16, m))


N, S, K, D = 2, 512, 512, 512


def scaled_scores(aq, bq, width):
    return (aq @ bq) / np.sqrt(width)


def softmax(x):
    e = np.exp(x - x.max(axis=-1, keepdims=True))
    return e / e.sum(axis=-1, keepdims=True)


def setup_inputs():
    s = mx_kscale(K)
    g = mx_kscale(D)
    t = mx_kscale(K)
    q = np.random.standard_normal((N, S, K))
    k = np.random.standard_normal((N, S, K))
    dk = np.random.standard_normal((N, S, K)) * 0.7
    v = np.random.standard_normal((N, S, K)) / np.sqrt(K)
    gres = np.random.standard_normal((S, D))
    wo = np.random.standard_normal((N, K, D)) / np.sqrt(D)
    return {"q": bf(q * s), "k": bf(k / s), "dk": bf(dk / s), "v": bf(v / t),
            "gres": bf(gres * g), "wo": bf(wo * t[None, :, None] / g[None, None, :])}


def core(q, k, dk, v, gres, wo):
    seq, width = q.shape[1], q.shape[2]

    qq = mxq(f64(q), 2, "e4m3")
    p = softmax(scaled_scores(qq, mxq(f64(k).transpose(0, 2, 1), 1, "e4m3"), width))
    d = scaled_scores(qq, mxq(f64(dk).transpose(0, 2, 1), 1, "e4m3"), width)

    go = mxq(f64(gres), 1, "e4m3") @ mxq(f64(wo).transpose(0, 2, 1), 1, "e4m3")
    ga = mxq(go, 2, "e4m3") @ mxq(f64(v).transpose(0, 2, 1), 1, "e4m3")

    gbar = np.sum(p * ga, axis=-1, keepdims=True)

    u = p * (np.exp(d) - 1.0)
    return seq * u * (ga - gbar) / (1.0 + u)


def reference(q, k, dk, v, gres, wo):
    R_out = core(q, k, dk, v, gres, wo)
    words, scales = planes(np.moveaxis(R_out, 1, 0).reshape(512, -1))
    return R_out, words, scales

@@ -1,0 +1,487 @@
+from contextlib import ExitStack
+
+import concourse.mybir as mybir
+from concourse.masks import make_identity
+
+HEADS, S, K = 2, 512, 512
+P = 128
+NT = 4
+SCALE = 1.0 / (512.0 ** 0.5)
+
+F32 = mybir.dt.float32
+BF16 = mybir.dt.bfloat16
+U32 = mybir.dt.uint32
+I32 = mybir.dt.int32
+U8 = mybir.dt.uint8
+FP8X4 = mybir.dt.float8_e4m3fn_x4
+ALU = mybir.AluOpType
+ACT = mybir.ActivationFunctionType
+AX = mybir.AxisListType
+
+FLOPS = 2 * 4 * 2 * S * S * K + 15 * HEADS * S * S
+
+
+def tile_atpstarsinglekeypatcheffect_x1_kernel(
+    tc, q, k, dk, v, gres, wo, out_0, out_1, out_2
+):
+    nc = tc.nc
+    with ExitStack() as ctx:
+        keep = ctx.enter_context(tc.tile_pool(name="keep", bufs=1))
+        work = ctx.enter_context(tc.tile_pool(name="work", bufs=4))
+        psum = ctx.enter_context(tc.psum_pool(name="psum", bufs=8))
+
+        def new_bank(shape):
+            bank = psum.tile(shape, F32, name="bank")
+            return bank
+
+        ident = keep.tile([P, P], F32, name="ident")
+        make_identity(nc, ident[:])
+        warm = keep.tile([P, 1], F32, name="warm")
+        nc.vector.memset(warm[:], 0.0)
+        nc.scalar.activation(out=warm[:], in_=warm[:], func=ACT.Exp)
+
+        raw = {}
+        grouped = {}
+        codes = {}
+        scales = {}
+
+        def load(name, src, blocked):
+            t = keep.tile([P, NT, K], BF16, name="raw_" + name)
+            raw[name] = t
+            if blocked:
+                view = src.rearrange("(t p) c -> p t c", p=P)
+            else:
+                view = src.rearrange("(p t) c -> p t c", t=NT)
+            for b in range(2):
+                nc.sync.dma_start(out=t[:, 2 * b : 2 * b + 2, :], in_=view[:, 2 * b : 2 * b + 2, :])
+
+        def turn(name, b):
+            bank = new_bank([P, 2, 2, P])
+            bank_t[name, b] = bank
+            for s in range(2):
+                words = raw[name][:, 2 * b + s, :].bitcast(F32)
+                for u in range(2):
+                    nc.tensor.transpose(bank[:, s, u, :], words[:, u : 2 * P : 2], ident[:])
+
+        def evac(name, b, eng):
+            if name not in grouped:
+                g = work.tile([P, S, NT], BF16, name="grouped", align_bytes=64, bufs=6)
+                grouped[name] = g
+            dst = grouped[name][:, 256 * b : 256 * b + 256, :].rearrange("p r j -> p (r j)").bitcast(F32)
+            dst = dst.rearrange("p (s r u) -> p s r u", s=2, u=2)
+            src = bank_t[name, b][:].rearrange("p s u r -> p s r u")
+            if eng == "S":
+                nc.scalar.copy(out=dst, in_=src)
+            else:
+                nc.vector.tensor_copy(out=dst, in_=src)
+
+        def quant(name, b):
+            if name not in codes:
+                c = keep.tile([P, S], U32, name="codes_" + name, align_bytes=64)
+                z = keep.tile([P, S], U8, name="scales_" + name, align_bytes=64)
+                codes[name] = c
+                scales[name] = z
+            nc.vector.quantize_mx(
+                out=codes[name][:, 256 * b : 256 * b + 256].bitcast(FP8X4),
+                scales=scales[name][:, 256 * b : 256 * b + 256],
+                in_=grouped[name][:, 256 * b : 256 * b + 256, :].rearrange("p r j -> p (r j)"),
+            )
+
+        def mm(dst, a, acols, b, bcols):
+            nc.tensor.matmul_mx(
+                out=dst,
+                lhsT=codes[a][:, acols].bitcast(FP8X4),
+                lhsT_scale=scales[a][:, acols],
+                rhs=codes[b][:, bcols].bitcast(FP8X4),
+                rhs_scale=scales[b][:, bcols],
+                start=True,
+                stop=True,
+            )
+
+        def sl(c):
+            return slice(P * c, P * c + P)
+
+        ALLC = slice(0, S)
+        zsum, rz, e_t, w_t, gw_t, bank_t, bank_s, bank_d, bank_go, nm_t, big_t, bank_ga, gb_t, r_t, ars_t, out_t = ({} for i in range(16))
+
+        def scores(h, t):
+            bank = new_bank([P, S])
+            bank_s[h, t] = bank
+            mm(bank[:], "q%d" % h, sl(t), "k%d" % h, ALLC)
+
+        def rowmax(h, t):
+            m = work.tile([P, 1], F32, name="m", bufs=8)
+            nc.vector.tensor_reduce(out=m[:], in_=bank_s[h, t][:], axis=AX.X, op=ALU.max)
+            nm = work.tile([P, 1], F32, name="nm", bufs=8)
+            nm_t[h, t] = nm
+            nc.gpsimd.tensor_scalar(out=nm[:], in0=m[:], scalar1=-SCALE, scalar2=0.0, op0=ALU.mult, op1=ALU.add)
+
+        def exp_s(h, t):
+            if h not in zsum:
+                zz = keep.tile([P, NT], F32, name="zsum%d" % h)
+                zsum[h] = zz
+            e = keep.tile([P, S], F32, name="e%d" % (4 * h + t))
+            e_t[h, t] = e
+            nc.scalar.activation(
+                out=e[:], in_=bank_s[h, t][:], func=ACT.Exp, bias=nm_t[h, t][:], scale=SCALE,
+                accum_out=zsum[h][:, t : t + 1],
+            )
+
+        def both(h, t):
+            bank = new_bank([P, S])
+            bank_d[h, t] = bank
+            for name, first in (("k%d" % h, True), ("dk%d" % h, False)):
+                nc.tensor.matmul_mx(
+                    out=bank[:],
+                    lhsT=codes["q%d" % h][:, sl(t)].bitcast(FP8X4),
+                    lhsT_scale=scales["q%d" % h][:, sl(t)],
+                    rhs=codes[name][:].bitcast(FP8X4),
+                    rhs_scale=scales[name][:],
+                    start=first,
+                    stop=not first,
+                )
+
+        def exp_b(h, t):
+            big = keep.tile([P, S], F32, name="big%d" % (4 * h + t))
+            big_t[h, t] = big
+            nc.scalar.activation(out=big[:], in_=bank_d[h, t][:], func=ACT.Exp, bias=nm_t[h, t][:], scale=SCALE)
+
+        def make_w(h, t, eng):
+            w = keep.tile([P, S], F32, name="w%d" % (4 * h + t))
+            w_t[h, t] = w
+            e = nc.gpsimd if eng == "G" else nc.vector
+            e.tensor_tensor(out=w[:], in0=big_t[h, t][:], in1=e_t[h, t][:], op=ALU.subtract)
+
+        def go_mm(h, c):
+            if ("go%d" % h) not in codes:
+                g = work.tile([P, S, NT], BF16, name="grouped", align_bytes=64, bufs=6)
+                grouped["go%d" % h] = g
+                cc = keep.tile([P, S], U32, name="codes_go%d" % h, align_bytes=64)
+                z = keep.tile([P, S], U8, name="scales_go%d" % h, align_bytes=64)
+                codes["go%d" % h] = cc
+                scales["go%d" % h] = z
+            bank = new_bank([P, NT, P])
+            bank_go[h, c] = bank
+            for j in range(NT):
+                mm(bank[:, j, :], "wo%d" % h, sl(j), "gres", sl(c))
+
+        def go_copy(h, c, eng):
+            dst = grouped["go%d" % h][:, sl(c), :]
+            src = bank_go[h, c][:].rearrange("p j n -> p n j")
+            if eng == "S":
+                nc.scalar.copy(out=dst, in_=src)
+            else:
+                nc.vector.tensor_copy(out=dst, in_=src)
+
+        def go_quant(h, c, n):
+            cols = slice(P * c, P * (c + n))
+            nc.vector.quantize_mx(
+                out=codes["go%d" % h][:, cols].bitcast(FP8X4),
+                scales=scales["go%d" % h][:, cols],
+                in_=grouped["go%d" % h][:, cols, :].rearrange("p r j -> p (r j)"),
+            )
+
+        def inv_z(h):
+            r = keep.tile([P, NT], F32, name="rz%d" % h)
+            rz[h] = r
+            nc.vector.reciprocal(r[:], zsum[h][:])
+
+        def ga_mm(h, t):
+            bank = new_bank([P, S])
+            bank_ga[h, t] = bank
+            mm(bank[:], "go%d" % h, sl(t), "v%d" % h, ALLC)
+
+        def ga_sum(h, t):
+            bank = bank_ga[h, t]
+            junk = work.tile([P, S], F32, name="junk")
+            gb = work.tile([P, 1], F32, name="gb", bufs=8)
+            gb_t[h, t] = gb
+            nc.vector.scalar_tensor_tensor(
+                out=junk[:], in0=bank[:], scalar=rz[h][:, t : t + 1], in1=e_t[h, t][:],
+                op0=ALU.mult, op1=ALU.mult, accum_out=gb[:],
+            )
+
+        def ga_w(h, t):
+            gw = keep.tile([P, S], F32, name="gw%d" % (4 * h + t))
+            gw_t[h, t] = gw
+            nc.vector.scalar_tensor_tensor(
+                out=gw[:], in0=bank_ga[h, t][:], scalar=gb_t[h, t][:], in1=w_t[h, t][:],
+                op0=ALU.subtract, op1=ALU.mult,
+            )
+
+        def recip_root(h, t, lo, n):
+            a = work.tile([P, S], F32, name="ars", bufs=6)
+            ars_t[h, t, lo] = a
+            nc.scalar.activation(
+                out=a[:, :n], in_=w_t[h, t][:, lo : lo + n], func=ACT.Abs_reciprocal_sqrt,
+                bias=zsum[h][:, t : t + 1], scale=1.0,
+            )
+
+        def recip_sq(h, t, lo, n):
+            r = work.tile([P, S], F32, name="r", bufs=6)
+            r_t[h, t, lo] = r
+            nc.scalar.activation(out=r[:, :n], in_=ars_t[h, t, lo][:, :n], func=ACT.Square, scale=512.0 ** 0.5)
+
+        def final(h, t, lo, n, eng):
+            if h not in out_t:
+                o = keep.tile([P, NT, S], F32, name="out%d" % h)
+                out_t[h] = o
+            o = out_t[h]
+            e = nc.gpsimd if eng == "G" else nc.vector
+            e.tensor_tensor(out=o[:, t, lo : lo + n], in0=gw_t[h, t][:, lo : lo + n], in1=r_t[h, t, lo][:, :n], op=ALU.mult)
+
+        def store(h, lo, n):
+            nc.sync.dma_start(
+                out=out_0[h].rearrange("(p t) j -> p t j", t=NT)[:, :, lo : lo + n], in_=out_t[h][:, :, lo : lo + n]
+            )
+
+        def spread(h, lo, n, eng):
+            if ("out%d" % h) not in codes:
+                g = work.tile([P, S, NT], BF16, name="grouped", align_bytes=64, bufs=6)
+                grouped["out%d" % h] = g
+                c = keep.tile([P, S], U32, name="ocodes%d" % h, align_bytes=64)
+                z = keep.tile([P, S], U8, name="oscales%d" % h, align_bytes=64)
+                codes["out%d" % h] = c
+                scales["out%d" % h] = z
+            dst = grouped["out%d" % h][:, lo : lo + n, :]
+            src = out_t[h][:, :, lo : lo + n].rearrange("p t j -> p j t")
+            if eng == "S":
+                nc.scalar.copy(out=dst, in_=src)
+            elif eng == "G":
+                nc.gpsimd.tensor_scalar(out=dst, in0=src, scalar1=1.0, scalar2=0.0, op0=ALU.mult, op1=ALU.add)
+            else:
+                nc.vector.tensor_copy(out=dst, in_=src)
+
+        def planes(h, lo, n):
+            c, z = codes["out%d" % h], scales["out%d" % h]
+            cols = slice(lo, lo + n)
+            nc.vector.quantize_mx(
+                out=c[:, cols].bitcast(FP8X4), scales=z[:, cols],
+                in_=grouped["out%d" % h][:, cols, :].rearrange("p r j -> p (r j)"),
+            )
+            ocols = slice(S * h + lo, S * h + lo + n)
+            nc.sync.dma_start(
+                out=out_1[0][:, ocols, :].rearrange("p m t -> p (m t)").bitcast(I32), in_=c[:, cols].bitcast(I32)
+            )
+            for qd in range(4):
+                nc.sync.dma_start(
+                    out=out_2[0, 4 * qd : 4 * qd + 4, ocols].bitcast(I32),
+                    in_=z[32 * qd : 32 * qd + 4, cols].bitcast(I32),
+                )
+
+        srcs = [("q0", q[0], False), ("k0", k[0], True), ("dk0", dk[0], True), ("gres", gres, False),
+                ("wo0", wo[0], False), ("v0", v[0], True), ("q1", q[1], False), ("k1", k[1], True),
+                ("dk1", dk[1], True), ("wo1", wo[1], False), ("v1", v[1], True)]
+
+        with tc.manual_schedule():
+            for name, src, blocked in srcs:
+                load(name, src, blocked)
+            turn("q0", 0)
+            turn("q0", 1)
+            evac("q0", 0, "S")
+            turn("k0", 0)
+            evac("q0", 1, "V")
+            turn("k0", 1)
+            quant("q0", 0)
+            evac("k0", 0, "S")
+            quant("q0", 1)
+            turn("dk0", 0)
+            evac("k0", 1, "S")
+            quant("k0", 0)
+            turn("dk0", 1)
+            quant("k0", 1)
+            evac("dk0", 0, "V")
+            turn("gres", 0)
+            evac("dk0", 1, "V")
+            scores(0, 1)
+            scores(0, 3)
+            quant("dk0", 0)
+            scores(0, 0)
+            evac("gres", 0, "V")
+            turn("wo0", 0)
+            quant("dk0", 1)
+            turn("wo0", 1)
+            rowmax(0, 3)
+            evac("wo0", 0, "S")
+            both(0, 0)
+            rowmax(0, 0)
+            evac("wo0", 1, "S")
+            rowmax(0, 1)
+            scores(0, 2)
+            exp_s(0, 3)
+            turn("q1", 0)
+            quant("wo0", 1)
+            exp_b(0, 0)
+            rowmax(0, 2)
+            turn("q1", 1)
+            exp_s(0, 1)
+            evac("q1", 0, "V")
+            turn("k1", 0)
+            exp_s(0, 2)
+            quant("gres", 0)
+            turn("gres", 1)
+            quant("q1", 0)
+            turn("k1", 1)
+            quant("wo0", 0)
+            evac("k1", 0, "S")
+            go_mm(0, 1)
+            evac("gres", 1, "S")
+            quant("k1", 0)
+            go_mm(0, 0)
+            evac("k1", 1, "V")
+            go_copy(0, 1, "S")
+            both(0, 3)
+            quant("gres", 1)
+            evac("q1", 1, "S")
+            both(0, 2)
+            quant("k1", 1)
+            go_quant(0, 1, 1)
+            exp_b(0, 3)
+            quant("q1", 1)
+            scores(1, 1)
+            go_mm(0, 2)
+            go_copy(0, 0, "S")
+            rowmax(1, 1)
+            make_w(0, 3, "G")
+            scores(1, 0)
+            scores(1, 2)
+            go_copy(0, 2, "S")
+            rowmax(1, 0)
+            scores(1, 3)
+            both(0, 1)
+            exp_s(0, 0)
+            rowmax(1, 2)
+            turn("wo1", 0)
+            go_quant(0, 2, 1)
+            exp_s(1, 0)
+            inv_z(0)
+            make_w(0, 0, "G")
+            rowmax(1, 3)
+            turn("dk1", 1)
+            exp_s(1, 2)
+            evac("wo1", 0, "V")
+            turn("wo1", 1)
+            exp_b(0, 1)
+            evac("dk1", 1, "V")
+            turn("v1", 1)
+            evac("wo1", 1, "S")
+            go_quant(0, 0, 1)
+            turn("dk1", 0)
+            make_w(0, 1, "V")
+            exp_s(1, 3)
+            go_mm(0, 3)
+            quant("dk1", 1)
+            quant("wo1", 1)
+            turn("v1", 0)
+            evac("dk1", 0, "S")
+            evac("v1", 1, "V")
+            exp_s(1, 1)
+            turn("v0", 0)
+            quant("dk1", 0)
+            quant("v1", 1)
+            turn("v0", 1)
+            evac("v1", 0, "S")
+            quant("wo1", 0)
+            inv_z(1)
+            both(1, 0)
+            evac("v0", 0, "S")
+            evac("v0", 1, "V")
+            go_copy(0, 3, "S")
+            go_mm(1, 2)
+            quant("v0", 0)
+            go_mm(1, 3)
+            quant("v0", 1)
+            exp_b(1, 0)
+            go_mm(1, 1)
+            go_quant(0, 3, 1)
+            quant("v1", 0)
+            ga_mm(0, 1)
+            go_copy(1, 3, "S")
+            go_copy(1, 1, "V")
+            make_w(1, 0, "G")
+            ga_mm(0, 3)
+            ga_mm(0, 2)
+            go_copy(1, 2, "S")
+            ga_sum(0, 1)
+            go_mm(1, 0)
+            both(1, 2)
+            exp_b(0, 2)
+            go_copy(1, 0, "V")
+            both(1, 1)
+            make_w(0, 2, "G")
+            exp_b(1, 2)
+            ga_w(0, 1)
+            both(1, 3)
+            exp_b(1, 1)
+            ga_sum(0, 2)
+            ga_mm(0, 0)
+            exp_b(1, 3)
+            make_w(1, 2, "G")
+            ga_sum(0, 3)
+            recip_root(0, 2, 0, 512)
+            ga_sum(0, 0)
+            make_w(1, 1, "G")
+            ga_w(0, 3)
+            ga_w(0, 0)
+            go_quant(1, 1, 1)
+            go_quant(1, 0, 1)
+            ga_mm(1, 1)
+            recip_root(0, 1, 0, 512)
+            go_quant(1, 2, 1)
+            go_quant(1, 3, 1)
+            ga_mm(1, 0)
+            ga_w(0, 2)
+            make_w(1, 3, "G")
+            ga_mm(1, 3)
+            recip_root(1, 0, 0, 256)
+            ga_mm(1, 2)
+            ga_sum(1, 0)
+            recip_sq(0, 1, 0, 512)
+            recip_root(0, 0, 0, 512)
+            ga_sum(1, 2)
+            final(0, 1, 0, 512, "G")
+            recip_sq(0, 2, 0, 512)
+            ga_w(1, 0)
+            recip_sq(0, 0, 0, 512)
+            ga_sum(1, 3)
+            final(0, 2, 0, 512, "G")
+            recip_root(1, 1, 0, 256)
+            ga_sum(1, 1)
+            recip_root(0, 3, 0, 512)
+            ga_w(1, 3)
+            final(0, 0, 0, 512, "G")
+            recip_sq(1, 1, 0, 256)
+            recip_sq(0, 3, 0, 512)
+            ga_w(1, 1)
+            recip_root(1, 2, 256, 256)
+            ga_w(1, 2)
+            final(1, 1, 0, 256, "G")
+            recip_root(1, 0, 256, 256)
+            recip_root(1, 1, 256, 256)
+            final(0, 3, 0, 512, "V")
+            store(0, 0, 512)
+            recip_sq(1, 2, 256, 256)
+            recip_sq(1, 1, 256, 256)
+            final(1, 2, 256, 256, "V")
+            recip_sq(1, 0, 256, 256)
+            final(1, 1, 256, 256, "V")
+            recip_root(1, 2, 0, 256)
+            final(1, 0, 256, 256, "V")
+            recip_root(1, 3, 0, 256)
+            spread(0, 0, 512, "V")
+            recip_sq(1, 2, 0, 256)
+            recip_sq(1, 3, 0, 256)
+            recip_root(1, 3, 256, 256)
+            recip_sq(1, 0, 0, 256)
+            final(1, 2, 0, 256, "V")
+            recip_sq(1, 3, 256, 256)
+            planes(0, 0, 512)
+            final(1, 0, 0, 256, "V")
+            final(1, 3, 256, 256, "V")
+            store(1, 256, 256)
+            final(1, 3, 0, 256, "V")
+            store(1, 0, 256)
+            spread(1, 256, 256, "V")
+            spread(1, 0, 256, "V")
+            planes(1, 256, 256)
+            planes(1, 0, 256)

@@ -36,6 +36,8 @@ def tile_atpstarsinglekeypatcheffect_x1_kernel(
 
         ident = keep.tile([P, P], F32, name="ident")
         make_identity(nc, ident[:])
+        zero = keep.tile([P, 256], F32, name="zero")
+        nc.vector.memset(zero[:], 0.0)
         warm = keep.tile([P, 1], F32, name="warm")
         nc.vector.memset(warm[:], 0.0)
         nc.scalar.activation(out=warm[:], in_=warm[:], func=ACT.Exp)
@@ -52,8 +54,13 @@ def tile_atpstarsinglekeypatcheffect_x1_kernel(
                 view = src.rearrange("(t p) c -> p t c", p=P)
             else:
                 view = src.rearrange("(p t) c -> p t c", t=NT)
-            for b in range(2):
-                nc.sync.dma_start(out=t[:, 2 * b : 2 * b + 2, :], in_=view[:, 2 * b : 2 * b + 2, :])
+            step = 1 if name == "q0" else 2
+            for b in range(0, NT, step):
+                nc.sync.dma_start(out=t[:, b : b + step, :], in_=view[:, b : b + step, :])
+
+        def dummy():
+            bank = new_bank([P, 256])
+            nc.tensor.matmul(bank[:], lhsT=zero[:, :P], rhs=zero[:], start=True, stop=True)
 
         def turn(name, b):
             bank = new_bank([P, 2, 2, P])
@@ -65,7 +72,7 @@ def tile_atpstarsinglekeypatcheffect_x1_kernel(
 
         def evac(name, b, eng):
             if name not in grouped:
-                g = work.tile([P, S, NT], BF16, name="grouped", align_bytes=64, bufs=6)
+                g = work.tile([P, S, NT], BF16, name="grouped", align_bytes=64, bufs=10)
                 grouped[name] = g
             dst = grouped[name][:, 256 * b : 256 * b + 256, :].rearrange("p r j -> p (r j)").bitcast(F32)
             dst = dst.rearrange("p (s r u) -> p s r u", s=2, u=2)
@@ -102,7 +109,7 @@ def tile_atpstarsinglekeypatcheffect_x1_kernel(
             return slice(P * c, P * c + P)
 
         ALLC = slice(0, S)
-        zsum, rz, e_t, w_t, gw_t, bank_t, bank_s, bank_d, bank_go, nm_t, big_t, bank_ga, gb_t, r_t, ars_t, out_t = ({} for i in range(16))
+        zsum, rz, e_t, w_t, gw_t, bank_t, bank_s, bank_d, bank_go, nm_t, big_t, bank_ga, gb_t, r_t, ars_t, out_t, mode, zs = ({} for i in range(18))
 
         def scores(h, t):
             bank = new_bank([P, S])
@@ -127,34 +134,44 @@ def tile_atpstarsinglekeypatcheffect_x1_kernel(
                 accum_out=zsum[h][:, t : t + 1],
             )
 
-        def both(h, t):
+        def shift(h, t, eng):
             bank = new_bank([P, S])
             bank_d[h, t] = bank
-            for name, first in (("k%d" % h, True), ("dk%d" % h, False)):
+            mode[h, t] = eng
+            names = ["k%d" % h, "dk%d" % h] if eng == "G" else ["dk%d" % h]
+            for name in names:
                 nc.tensor.matmul_mx(
                     out=bank[:],
                     lhsT=codes["q%d" % h][:, sl(t)].bitcast(FP8X4),
                     lhsT_scale=scales["q%d" % h][:, sl(t)],
                     rhs=codes[name][:].bitcast(FP8X4),
                     rhs_scale=scales[name][:],
-                    start=first,
-                    stop=not first,
+                    start=(name == names[0]),
+                    stop=(name == names[-1]),
                 )
 
         def exp_b(h, t):
             big = keep.tile([P, S], F32, name="big%d" % (4 * h + t))
             big_t[h, t] = big
-            nc.scalar.activation(out=big[:], in_=bank_d[h, t][:], func=ACT.Exp, bias=nm_t[h, t][:], scale=SCALE)
+            if mode[h, t] == "G":
+                nc.scalar.activation(out=big[:], in_=bank_d[h, t][:], func=ACT.Exp, bias=nm_t[h, t][:], scale=SCALE)
+            else:
+                nc.scalar.activation(out=big[:], in_=bank_d[h, t][:], func=ACT.Exp, scale=SCALE)
 
         def make_w(h, t, eng):
             w = keep.tile([P, S], F32, name="w%d" % (4 * h + t))
             w_t[h, t] = w
-            e = nc.gpsimd if eng == "G" else nc.vector
-            e.tensor_tensor(out=w[:], in0=big_t[h, t][:], in1=e_t[h, t][:], op=ALU.subtract)
+            if mode[h, t] == "G":
+                e = nc.gpsimd if eng == "G" else nc.vector
+                e.tensor_tensor(out=w[:], in0=big_t[h, t][:], in1=e_t[h, t][:], op=ALU.subtract)
+            else:
+                nc.vector.scalar_tensor_tensor(
+                    out=w[:], in0=big_t[h, t][:], scalar=-1.0, in1=e_t[h, t][:], op0=ALU.add, op1=ALU.mult
+                )
 
         def go_mm(h, c):
             if ("go%d" % h) not in codes:
-                g = work.tile([P, S, NT], BF16, name="grouped", align_bytes=64, bufs=6)
+                g = work.tile([P, S, NT], BF16, name="grouped", align_bytes=64, bufs=10)
                 grouped["go%d" % h] = g
                 cc = keep.tile([P, S], U32, name="codes_go%d" % h, align_bytes=64)
                 z = keep.tile([P, S], U8, name="scales_go%d" % h, align_bytes=64)
@@ -185,6 +202,9 @@ def tile_atpstarsinglekeypatcheffect_x1_kernel(
             r = keep.tile([P, NT], F32, name="rz%d" % h)
             rz[h] = r
             nc.vector.reciprocal(r[:], zsum[h][:])
+            zz = keep.tile([P, NT], F32, name="zs%d" % h)
+            zs[h] = zz
+            nc.vector.tensor_scalar(out=zz[:], in0=zsum[h][:], scalar1=1.0 / 512.0, scalar2=None, op0=ALU.mult)
 
         def ga_mm(h, t):
             bank = new_bank([P, S])
@@ -193,7 +213,7 @@ def tile_atpstarsinglekeypatcheffect_x1_kernel(
 
         def ga_sum(h, t):
             bank = bank_ga[h, t]
-            junk = work.tile([P, S], F32, name="junk")
+            junk = work.tile([P, S], F32, name="junk", bufs=2)
             gb = work.tile([P, 1], F32, name="gb", bufs=8)
             gb_t[h, t] = gb
             nc.vector.scalar_tensor_tensor(
@@ -214,37 +234,41 @@ def tile_atpstarsinglekeypatcheffect_x1_kernel(
             ars_t[h, t, lo] = a
             nc.scalar.activation(
                 out=a[:, :n], in_=w_t[h, t][:, lo : lo + n], func=ACT.Abs_reciprocal_sqrt,
-                bias=zsum[h][:, t : t + 1], scale=1.0,
+                bias=zs[h][:, t : t + 1], scale=1.0 / 512.0,
             )
 
-        def recip_sq(h, t, lo, n):
+        def recip_sq(h, t, lo, n, eng):
             r = work.tile([P, S], F32, name="r", bufs=6)
             r_t[h, t, lo] = r
-            nc.scalar.activation(out=r[:, :n], in_=ars_t[h, t, lo][:, :n], func=ACT.Square, scale=512.0 ** 0.5)
+            a = ars_t[h, t, lo]
+            if eng == "G":
+                nc.gpsimd.tensor_tensor(out=r[:, :n], in0=a[:, :n], in1=a[:, :n], op=ALU.mult)
+            else:
+                nc.scalar.activation(out=r[:, :n], in_=a[:, :n], func=ACT.Square)
 
         def final(h, t, lo, n, eng):
-            if h not in out_t:
-                o = keep.tile([P, NT, S], F32, name="out%d" % h)
-                out_t[h] = o
-            o = out_t[h]
+            if (h, lo) not in out_t:
+                o = keep.tile([P, NT, n], F32, name="out%d_%d" % (h, lo))
+                out_t[h, lo] = o
+            o = out_t[h, lo]
             e = nc.gpsimd if eng == "G" else nc.vector
-            e.tensor_tensor(out=o[:, t, lo : lo + n], in0=gw_t[h, t][:, lo : lo + n], in1=r_t[h, t, lo][:, :n], op=ALU.mult)
+            e.tensor_tensor(out=o[:, t, :], in0=gw_t[h, t][:, lo : lo + n], in1=r_t[h, t, lo][:, :n], op=ALU.mult)
 
         def store(h, lo, n):
             nc.sync.dma_start(
-                out=out_0[h].rearrange("(p t) j -> p t j", t=NT)[:, :, lo : lo + n], in_=out_t[h][:, :, lo : lo + n]
+                out=out_0[h].rearrange("(p t) j -> p t j", t=NT)[:, :, lo : lo + n], in_=out_t[h, lo][:]
             )
 
         def spread(h, lo, n, eng):
             if ("out%d" % h) not in codes:
-                g = work.tile([P, S, NT], BF16, name="grouped", align_bytes=64, bufs=6)
+                g = work.tile([P, S, NT], BF16, name="grouped", align_bytes=64, bufs=10)
                 grouped["out%d" % h] = g
                 c = keep.tile([P, S], U32, name="ocodes%d" % h, align_bytes=64)
                 z = keep.tile([P, S], U8, name="oscales%d" % h, align_bytes=64)
                 codes["out%d" % h] = c
                 scales["out%d" % h] = z
             dst = grouped["out%d" % h][:, lo : lo + n, :]
-            src = out_t[h][:, :, lo : lo + n].rearrange("p t j -> p j t")
+            src = out_t[h, lo][:].rearrange("p t j -> p j t")
             if eng == "S":
                 nc.scalar.copy(out=dst, in_=src)
             elif eng == "G":
@@ -254,234 +278,252 @@ def tile_atpstarsinglekeypatcheffect_x1_kernel(
 
         def planes(h, lo, n):
             c, z = codes["out%d" % h], scales["out%d" % h]
+            w = 512
+            at = lo
+            while at < lo + n:
+                while w > lo + n - at:
+                    w = w // 2
+                cols = slice(at, at + w)
+                nc.vector.quantize_mx(
+                    out=c[:, cols].bitcast(FP8X4), scales=z[:, cols],
+                    in_=grouped["out%d" % h][:, cols, :].rearrange("p r j -> p (r j)"),
+                )
+                at = at + w
             cols = slice(lo, lo + n)
-            nc.vector.quantize_mx(
-                out=c[:, cols].bitcast(FP8X4), scales=z[:, cols],
-                in_=grouped["out%d" % h][:, cols, :].rearrange("p r j -> p (r j)"),
-            )
             ocols = slice(S * h + lo, S * h + lo + n)
             nc.sync.dma_start(
                 out=out_1[0][:, ocols, :].rearrange("p m t -> p (m t)").bitcast(I32), in_=c[:, cols].bitcast(I32)
             )
-            for qd in range(4):
-                nc.sync.dma_start(
-                    out=out_2[0, 4 * qd : 4 * qd + 4, ocols].bitcast(I32),
-                    in_=z[32 * qd : 32 * qd + 4, cols].bitcast(I32),
-                )
+            if lo + n == S:
+                cols = slice(S * h, S * h + S)
+                for qd in range(4):
+                    q_ = nc.scalar if (h == 1 and qd % 2) else nc.sync
+                    q_.dma_start(
+                        out=out_2[0, 4 * qd : 4 * qd + 4, cols].bitcast(I32),
+                        in_=z[32 * qd : 32 * qd + 4, :].bitcast(I32),
+                    )
 
-        srcs = [("q0", q[0], False), ("k0", k[0], True), ("dk0", dk[0], True), ("gres", gres, False),
-                ("wo0", wo[0], False), ("v0", v[0], True), ("q1", q[1], False), ("k1", k[1], True),
-                ("dk1", dk[1], True), ("wo1", wo[1], False), ("v1", v[1], True)]
+        srcs = {"q0": (q[0], False), "k0": (k[0], True), "dk0": (dk[0], True), "gres": (gres, False),
+                "wo0": (wo[0], False), "v0": (v[0], True), "q1": (q[1], False), "k1": (k[1], True),
+                "dk1": (dk[1], True), "wo1": (wo[1], False), "v1": (v[1], True)}
 
         with tc.manual_schedule():
-            for name, src, blocked in srcs:
-                load(name, src, blocked)
+            for name in ("q0", "k0", "dk0", "gres", "wo0", "v0", "q1", "k1", "dk1", "wo1", "v1"):
+                load(name, *srcs[name])
+            dummy()
+            dummy()
             turn("q0", 0)
-            turn("q0", 1)
+            dummy()
             evac("q0", 0, "S")
-            turn("k0", 0)
-            evac("q0", 1, "V")
-            turn("k0", 1)
+            turn("q0", 1)
             quant("q0", 0)
-            evac("k0", 0, "S")
-            quant("q0", 1)
+            turn("k0", 0)
+            evac("q0", 1, "S")
+            turn("k0", 1)
+            evac("k0", 0, "V")
+            dummy()
+            evac("k0", 1, "V")
             turn("dk0", 0)
-            evac("k0", 1, "S")
-            quant("k0", 0)
+            quant("q0", 1)
             turn("dk0", 1)
-            quant("k0", 1)
             evac("dk0", 0, "V")
-            turn("gres", 0)
-            evac("dk0", 1, "V")
-            scores(0, 1)
-            scores(0, 3)
-            quant("dk0", 0)
-            scores(0, 0)
-            evac("gres", 0, "V")
-            turn("wo0", 0)
-            quant("dk0", 1)
-            turn("wo0", 1)
-            rowmax(0, 3)
-            evac("wo0", 0, "S")
-            both(0, 0)
-            rowmax(0, 0)
-            evac("wo0", 1, "S")
-            rowmax(0, 1)
-            scores(0, 2)
-            exp_s(0, 3)
-            turn("q1", 0)
-            quant("wo0", 1)
-            exp_b(0, 0)
-            rowmax(0, 2)
-            turn("q1", 1)
-            exp_s(0, 1)
-            evac("q1", 0, "V")
-            turn("k1", 0)
-            exp_s(0, 2)
-            quant("gres", 0)
             turn("gres", 1)
-            quant("q1", 0)
-            turn("k1", 1)
-            quant("wo0", 0)
-            evac("k1", 0, "S")
-            go_mm(0, 1)
-            evac("gres", 1, "S")
-            quant("k1", 0)
-            go_mm(0, 0)
-            evac("k1", 1, "V")
-            go_copy(0, 1, "S")
-            both(0, 3)
+            quant("k0", 0)
+            quant("dk0", 0)
+            turn("gres", 0)
+            quant("k0", 1)
+            turn("wo0", 1)
+            evac("gres", 1, "V")
+            evac("gres", 0, "V")
+            dummy()
+            evac("dk0", 1, "V")
+            evac("wo0", 1, "S")
+            quant("wo0", 1)
+            turn("v0", 1)
+            quant("gres", 0)
+            quant("dk0", 1)
+            turn("wo0", 0)
             quant("gres", 1)
+            dummy()
+            evac("wo0", 0, "S")
+            turn("q1", 1)
+            quant("wo0", 0)
+            turn("k1", 0)
             evac("q1", 1, "S")
-            both(0, 2)
-            quant("k1", 1)
-            go_quant(0, 1, 1)
-            exp_b(0, 3)
+            scores(0, 2)
+            evac("k1", 0, "S")
+            scores(0, 1)
+            rowmax(0, 2)
+            turn("dk1", 0)
+            evac("v0", 1, "S")
+            quant("k1", 0)
+            turn("k1", 1)
             quant("q1", 1)
-            scores(1, 1)
+            evac("dk1", 0, "S")
+            rowmax(0, 1)
+            turn("dk1", 1)
+            evac("k1", 1, "S")
+            turn("wo1", 1)
+            evac("dk1", 1, "S")
+            quant("k1", 1)
             go_mm(0, 2)
-            go_copy(0, 0, "S")
-            rowmax(1, 1)
+            quant("dk1", 0)
+            evac("wo1", 1, "S")
+            quant("dk1", 1)
+            go_mm(0, 1)
+            go_copy(0, 2, "V")
+            scores(0, 3)
+            exp_s(0, 1)
+            scores(0, 0)
+            quant("wo1", 1)
+            turn("wo1", 0)
+            exp_s(0, 2)
+            rowmax(0, 3)
+            turn("q1", 0)
+            go_copy(0, 1, "S")
+            go_quant(0, 2, 1)
+            shift(0, 3, "G")
+            evac("wo1", 0, "S")
+            evac("q1", 0, "V")
+            turn("v1", 0)
+            exp_s(0, 3)
+            quant("wo1", 0)
+            rowmax(0, 0)
+            go_mm(1, 1)
+            exp_b(0, 3)
+            quant("q1", 0)
+            go_mm(1, 0)
+            go_copy(1, 1, "S")
+            evac("v1", 0, "V")
             make_w(0, 3, "G")
-            scores(1, 0)
             scores(1, 2)
-            go_copy(0, 2, "S")
+            shift(0, 2, "V")
+            go_copy(1, 0, "S")
+            rowmax(1, 2)
+            scores(1, 1)
+            scores(1, 0)
+            exp_b(0, 2)
+            rowmax(1, 1)
+            go_mm(1, 3)
+            shift(0, 1, "G")
+            exp_s(1, 2)
+            go_quant(1, 1, 1)
             rowmax(1, 0)
             scores(1, 3)
-            both(0, 1)
-            exp_s(0, 0)
-            rowmax(1, 2)
-            turn("wo1", 0)
-            go_quant(0, 2, 1)
-            exp_s(1, 0)
-            inv_z(0)
-            make_w(0, 0, "G")
-            rowmax(1, 3)
-            turn("dk1", 1)
-            exp_s(1, 2)
-            evac("wo1", 0, "V")
-            turn("wo1", 1)
             exp_b(0, 1)
-            evac("dk1", 1, "V")
-            turn("v1", 1)
-            evac("wo1", 1, "S")
-            go_quant(0, 0, 1)
-            turn("dk1", 0)
-            make_w(0, 1, "V")
-            exp_s(1, 3)
             go_mm(0, 3)
-            quant("dk1", 1)
-            quant("wo1", 1)
-            turn("v1", 0)
-            evac("dk1", 0, "S")
-            evac("v1", 1, "V")
-            exp_s(1, 1)
-            turn("v0", 0)
-            quant("dk1", 0)
-            quant("v1", 1)
-            turn("v0", 1)
-            evac("v1", 0, "S")
-            quant("wo1", 0)
-            inv_z(1)
-            both(1, 0)
-            evac("v0", 0, "S")
-            evac("v0", 1, "V")
+            quant("v1", 0)
+            shift(0, 0, "G")
+            go_copy(1, 3, "V")
+            exp_s(0, 0)
+            make_w(0, 1, "G")
+            go_mm(0, 0)
+            rowmax(1, 3)
             go_copy(0, 3, "S")
             go_mm(1, 2)
-            quant("v0", 0)
-            go_mm(1, 3)
+            go_copy(0, 0, "V")
+            shift(1, 2, "V")
+            exp_b(0, 0)
+            turn("v0", 0)
+            make_w(0, 2, "V")
+            exp_s(1, 3)
+            turn("v1", 1)
+            go_copy(1, 2, "V")
+            make_w(0, 0, "G")
+            evac("v0", 0, "S")
+            shift(1, 0, "G")
+            inv_z(0)
+            evac("v1", 1, "V")
+            exp_s(1, 0)
+            shift(1, 1, "G")
             quant("v0", 1)
-            exp_b(1, 0)
-            go_mm(1, 1)
-            go_quant(0, 3, 1)
-            quant("v1", 0)
-            ga_mm(0, 1)
-            go_copy(1, 3, "S")
-            go_copy(1, 1, "V")
-            make_w(1, 0, "G")
-            ga_mm(0, 3)
-            ga_mm(0, 2)
-            go_copy(1, 2, "S")
-            ga_sum(0, 1)
-            go_mm(1, 0)
-            both(1, 2)
-            exp_b(0, 2)
-            go_copy(1, 0, "V")
-            both(1, 1)
-            make_w(0, 2, "G")
-            exp_b(1, 2)
-            ga_w(0, 1)
-            both(1, 3)
+            exp_s(1, 1)
+            quant("v0", 0)
+            shift(1, 3, "G")
+            go_quant(1, 0, 1)
+            go_quant(0, 1, 1)
+            go_quant(0, 0, 1)
             exp_b(1, 1)
-            ga_sum(0, 2)
+            ga_mm(0, 1)
+            quant("v1", 1)
             ga_mm(0, 0)
-            exp_b(1, 3)
-            make_w(1, 2, "G")
-            ga_sum(0, 3)
-            recip_root(0, 2, 0, 512)
+            inv_z(1)
+            go_quant(1, 2, 1)
+            exp_b(1, 0)
+            go_quant(0, 3, 1)
+            go_quant(1, 3, 1)
+            ga_mm(0, 3)
             ga_sum(0, 0)
             make_w(1, 1, "G")
-            ga_w(0, 3)
-            ga_w(0, 0)
-            go_quant(1, 1, 1)
-            go_quant(1, 0, 1)
-            ga_mm(1, 1)
-            recip_root(0, 1, 0, 512)
-            go_quant(1, 2, 1)
-            go_quant(1, 3, 1)
-            ga_mm(1, 0)
-            ga_w(0, 2)
-            make_w(1, 3, "G")
+            exp_b(1, 3)
             ga_mm(1, 3)
-            recip_root(1, 0, 0, 256)
+            ga_mm(1, 0)
+            ga_sum(0, 3)
+            exp_b(1, 2)
+            ga_mm(0, 2)
             ga_mm(1, 2)
-            ga_sum(1, 0)
-            recip_sq(0, 1, 0, 512)
+            make_w(1, 3, "G")
             recip_root(0, 0, 0, 512)
-            ga_sum(1, 2)
-            final(0, 1, 0, 512, "G")
-            recip_sq(0, 2, 0, 512)
-            ga_w(1, 0)
-            recip_sq(0, 0, 0, 512)
-            ga_sum(1, 3)
-            final(0, 2, 0, 512, "G")
-            recip_root(1, 1, 0, 256)
+            ga_w(0, 0)
+            dummy()
+            ga_sum(1, 0)
+            ga_mm(1, 1)
+            make_w(1, 0, "G")
+            ga_sum(0, 1)
+            dummy()
+            ga_sum(0, 2)
+            recip_root(1, 1, 0, 384)
+            recip_sq(0, 0, 0, 512, "G")
             ga_sum(1, 1)
-            recip_root(0, 3, 0, 512)
-            ga_w(1, 3)
+            recip_root(1, 0, 384, 128)
+            recip_root(0, 2, 0, 512)
+            ga_w(0, 1)
+            recip_sq(1, 0, 384, 128, "S")
+            make_w(1, 2, "V")
+            recip_root(0, 1, 0, 512)
+            ga_w(1, 0)
             final(0, 0, 0, 512, "G")
-            recip_sq(1, 1, 0, 256)
-            recip_sq(0, 3, 0, 512)
+            recip_root(1, 1, 384, 128)
+            recip_root(1, 2, 384, 128)
+            recip_root(1, 3, 384, 128)
+            ga_sum(1, 3)
+            recip_sq(1, 1, 0, 384, "S")
+            recip_root(0, 3, 0, 512)
             ga_w(1, 1)
-            recip_root(1, 2, 256, 256)
+            final(1, 0, 384, 128, "G")
+            recip_sq(1, 1, 384, 128, "G")
+            recip_sq(0, 1, 0, 512, "S")
+            ga_sum(1, 2)
+            recip_sq(1, 3, 384, 128, "G")
+            recip_root(1, 3, 0, 384)
+            ga_w(0, 3)
+            final(0, 1, 0, 512, "G")
+            recip_root(1, 2, 0, 384)
+            ga_w(0, 2)
+            recip_sq(0, 2, 0, 512, "S")
+            ga_w(1, 3)
+            final(1, 1, 0, 384, "G")
+            recip_sq(1, 2, 384, 128, "S")
+            recip_sq(0, 3, 0, 512, "S")
             ga_w(1, 2)
-            final(1, 1, 0, 256, "G")
-            recip_root(1, 0, 256, 256)
-            recip_root(1, 1, 256, 256)
+            recip_root(1, 0, 0, 384)
+            final(0, 2, 0, 512, "V")
+            recip_sq(1, 2, 0, 384, "S")
             final(0, 3, 0, 512, "V")
             store(0, 0, 512)
-            recip_sq(1, 2, 256, 256)
-            recip_sq(1, 1, 256, 256)
-            final(1, 2, 256, 256, "V")
-            recip_sq(1, 0, 256, 256)
-            final(1, 1, 256, 256, "V")
-            recip_root(1, 2, 0, 256)
-            final(1, 0, 256, 256, "V")
-            recip_root(1, 3, 0, 256)
-            spread(0, 0, 512, "V")
-            recip_sq(1, 2, 0, 256)
-            recip_sq(1, 3, 0, 256)
-            recip_root(1, 3, 256, 256)
-            recip_sq(1, 0, 0, 256)
-            final(1, 2, 0, 256, "V")
-            recip_sq(1, 3, 256, 256)
+            recip_sq(1, 0, 0, 384, "S")
+            final(1, 2, 0, 384, "V")
+            recip_sq(1, 3, 0, 384, "S")
+            final(1, 3, 384, 128, "V")
+            spread(0, 0, 512, "S")
+            final(1, 3, 0, 384, "V")
+            final(1, 0, 0, 384, "V")
+            store(1, 0, 384)
+            final(1, 1, 384, 128, "V")
+            final(1, 2, 384, 128, "V")
+            store(1, 384, 128)
+            spread(1, 0, 384, "V")
+            spread(1, 384, 128, "S")
             planes(0, 0, 512)
-            final(1, 0, 0, 256, "V")
-            final(1, 3, 256, 256, "V")
-            store(1, 256, 256)
-            final(1, 3, 0, 256, "V")
-            store(1, 0, 256)
-            spread(1, 256, 256, "V")
-            spread(1, 0, 256, "V")
-            planes(1, 256, 256)
-            planes(1, 0, 256)
+            planes(1, 0, 384)
+            planes(1, 384, 128)

@@ -316,214 +316,212 @@ def tile_atpstarsinglekeypatcheffect_x1_kernel(
             dummy()
             evac("q0", 0, "S")
             turn("q0", 1)
-            quant("q0", 0)
             turn("k0", 0)
-            evac("q0", 1, "S")
+            evac("q0", 1, "V")
             turn("k0", 1)
-            evac("k0", 0, "V")
-            dummy()
-            evac("k0", 1, "V")
-            turn("dk0", 0)
+            evac("k0", 0, "S")
             quant("q0", 1)
-            turn("dk0", 1)
-            evac("dk0", 0, "V")
-            turn("gres", 1)
-            quant("k0", 0)
-            quant("dk0", 0)
-            turn("gres", 0)
+            dummy()
+            evac("k0", 1, "S")
+            quant("q0", 0)
+            turn("dk0", 0)
             quant("k0", 1)
-            turn("wo0", 1)
-            evac("gres", 1, "V")
-            evac("gres", 0, "V")
+            turn("dk0", 1)
+            quant("k0", 0)
+            evac("dk0", 0, "S")
+            turn("gres", 1)
+            evac("dk0", 1, "S")
+            turn("gres", 0)
+            evac("gres", 1, "S")
             dummy()
-            evac("dk0", 1, "V")
-            evac("wo0", 1, "S")
-            quant("wo0", 1)
-            turn("v0", 1)
-            quant("gres", 0)
-            quant("dk0", 1)
-            turn("wo0", 0)
+            evac("gres", 0, "S")
             quant("gres", 1)
-            dummy()
+            quant("dk0", 0)
+            quant("gres", 0)
+            turn("wo0", 0)
+            quant("dk0", 1)
+            turn("wo0", 1)
             evac("wo0", 0, "S")
-            turn("q1", 1)
-            quant("wo0", 0)
-            turn("k1", 0)
-            evac("q1", 1, "S")
-            scores(0, 2)
-            evac("k1", 0, "S")
-            scores(0, 1)
-            rowmax(0, 2)
-            turn("dk1", 0)
-            evac("v0", 1, "S")
-            quant("k1", 0)
-            turn("k1", 1)
-            quant("q1", 1)
-            evac("dk1", 0, "S")
-            rowmax(0, 1)
-            turn("dk1", 1)
-            evac("k1", 1, "S")
-            turn("wo1", 1)
-            evac("dk1", 1, "S")
-            quant("k1", 1)
-            go_mm(0, 2)
-            quant("dk1", 0)
-            evac("wo1", 1, "S")
-            quant("dk1", 1)
-            go_mm(0, 1)
-            go_copy(0, 2, "V")
             scores(0, 3)
-            exp_s(0, 1)
-            scores(0, 0)
-            quant("wo1", 1)
-            turn("wo1", 0)
-            exp_s(0, 2)
+            evac("wo0", 1, "S")
+            quant("wo0", 0)
+            scores(0, 1)
             rowmax(0, 3)
+            scores(0, 2)
+            scores(0, 0)
+            rowmax(0, 1)
             turn("q1", 0)
-            go_copy(0, 1, "S")
-            go_quant(0, 2, 1)
-            shift(0, 3, "G")
-            evac("wo1", 0, "S")
-            evac("q1", 0, "V")
-            turn("v1", 0)
             exp_s(0, 3)
-            quant("wo1", 0)
+            rowmax(0, 2)
+            turn("k1", 1)
+            exp_s(0, 1)
             rowmax(0, 0)
-            go_mm(1, 1)
-            exp_b(0, 3)
-            quant("q1", 0)
-            go_mm(1, 0)
-            go_copy(1, 1, "S")
-            evac("v1", 0, "V")
-            make_w(0, 3, "G")
-            scores(1, 2)
-            shift(0, 2, "V")
-            go_copy(1, 0, "S")
-            rowmax(1, 2)
-            scores(1, 1)
-            scores(1, 0)
-            exp_b(0, 2)
-            rowmax(1, 1)
-            go_mm(1, 3)
-            shift(0, 1, "G")
-            exp_s(1, 2)
-            go_quant(1, 1, 1)
-            rowmax(1, 0)
-            scores(1, 3)
-            exp_b(0, 1)
-            go_mm(0, 3)
-            quant("v1", 0)
-            shift(0, 0, "G")
-            go_copy(1, 3, "V")
+            turn("k1", 0)
+            evac("q1", 0, "S")
+            evac("k1", 1, "V")
+            dummy()
+            exp_s(0, 2)
+            evac("k1", 0, "V")
+            turn("q1", 1)
             exp_s(0, 0)
-            make_w(0, 1, "G")
-            go_mm(0, 0)
-            rowmax(1, 3)
-            go_copy(0, 3, "S")
-            go_mm(1, 2)
-            go_copy(0, 0, "V")
-            shift(1, 2, "V")
-            exp_b(0, 0)
+            quant("wo0", 1)
             turn("v0", 0)
-            make_w(0, 2, "V")
-            exp_s(1, 3)
-            turn("v1", 1)
-            go_copy(1, 2, "V")
-            make_w(0, 0, "G")
+            quant("k1", 0)
+            evac("q1", 1, "S")
+            quant("q1", 0)
+            go_mm(0, 1)
+            quant("k1", 1)
+            turn("dk1", 0)
             evac("v0", 0, "S")
-            shift(1, 0, "G")
             inv_z(0)
-            evac("v1", 1, "V")
-            exp_s(1, 0)
-            shift(1, 1, "G")
-            quant("v0", 1)
-            exp_s(1, 1)
+            quant("q1", 1)
+            go_copy(0, 1, "V")
+            shift(0, 2, "V")
+            evac("dk1", 0, "S")
+            scores(1, 3)
             quant("v0", 0)
-            shift(1, 3, "G")
-            go_quant(1, 0, 1)
+            shift(0, 3, "V")
             go_quant(0, 1, 1)
-            go_quant(0, 0, 1)
-            exp_b(1, 1)
-            ga_mm(0, 1)
-            quant("v1", 1)
-            ga_mm(0, 0)
-            inv_z(1)
-            go_quant(1, 2, 1)
-            exp_b(1, 0)
+            exp_b(0, 2)
+            rowmax(1, 3)
+            go_mm(0, 2)
+            scores(1, 1)
+            exp_b(0, 3)
+            make_w(0, 2, "V")
+            shift(0, 1, "V")
+            scores(1, 2)
+            go_copy(0, 2, "S")
+            rowmax(1, 1)
+            scores(1, 0)
+            turn("dk1", 1)
+            exp_b(0, 1)
+            quant("dk1", 0)
+            rowmax(1, 0)
+            exp_s(1, 1)
+            turn("wo1", 0)
+            make_w(0, 1, "V")
+            go_mm(0, 0)
+            evac("dk1", 1, "S")
+            make_w(0, 3, "V")
+            go_mm(0, 3)
+            exp_s(1, 0)
+            turn("v0", 1)
+            quant("dk1", 1)
+            go_copy(0, 3, "S")
+            rowmax(1, 2)
+            turn("wo1", 1)
+            evac("wo1", 0, "S")
+            evac("v0", 1, "V")
+            shift(1, 2, "V")
+            shift(1, 0, "V")
+            evac("wo1", 1, "S")
             go_quant(0, 3, 1)
-            go_quant(1, 3, 1)
+            go_quant(0, 2, 1)
+            shift(1, 3, "V")
+            quant("v0", 1)
+            turn("v1", 0)
+            exp_s(1, 2)
+            go_copy(0, 0, "V")
             ga_mm(0, 3)
-            ga_sum(0, 0)
-            make_w(1, 1, "G")
+            quant("wo1", 0)
             exp_b(1, 3)
-            ga_mm(1, 3)
-            ga_mm(1, 0)
+            quant("wo1", 1)
+            shift(1, 1, "V")
+            exp_s(1, 3)
+            go_quant(0, 0, 1)
+            go_mm(1, 3)
             ga_sum(0, 3)
-            exp_b(1, 2)
-            ga_mm(0, 2)
-            ga_mm(1, 2)
-            make_w(1, 3, "G")
-            recip_root(0, 0, 0, 512)
-            ga_w(0, 0)
-            dummy()
-            ga_sum(1, 0)
-            ga_mm(1, 1)
-            make_w(1, 0, "G")
-            ga_sum(0, 1)
-            dummy()
-            ga_sum(0, 2)
-            recip_root(1, 1, 0, 384)
-            recip_sq(0, 0, 0, 512, "G")
-            ga_sum(1, 1)
-            recip_root(1, 0, 384, 128)
-            recip_root(0, 2, 0, 512)
-            ga_w(0, 1)
-            recip_sq(1, 0, 384, 128, "S")
-            make_w(1, 2, "V")
-            recip_root(0, 1, 0, 512)
-            ga_w(1, 0)
-            final(0, 0, 0, 512, "G")
-            recip_root(1, 1, 384, 128)
-            recip_root(1, 2, 384, 128)
-            recip_root(1, 3, 384, 128)
-            ga_sum(1, 3)
-            recip_sq(1, 1, 0, 384, "S")
-            recip_root(0, 3, 0, 512)
-            ga_w(1, 1)
-            final(1, 0, 384, 128, "G")
-            recip_sq(1, 1, 384, 128, "G")
-            recip_sq(0, 1, 0, 512, "S")
-            ga_sum(1, 2)
-            recip_sq(1, 3, 384, 128, "G")
-            recip_root(1, 3, 0, 384)
+            go_mm(1, 1)
+            evac("v1", 0, "S")
+            turn("v1", 1)
+            inv_z(1)
+            make_w(1, 3, "V")
+            go_copy(1, 1, "S")
+            shift(0, 0, "V")
             ga_w(0, 3)
-            final(0, 1, 0, 512, "G")
-            recip_root(1, 2, 0, 384)
-            ga_w(0, 2)
-            recip_sq(0, 2, 0, 512, "S")
-            ga_w(1, 3)
-            final(1, 1, 0, 384, "G")
-            recip_sq(1, 2, 384, 128, "S")
-            recip_sq(0, 3, 0, 512, "S")
-            ga_w(1, 2)
+            evac("v1", 1, "S")
+            ga_mm(0, 1)
+            go_quant(1, 1, 1)
+            ga_mm(0, 2)
+            quant("v1", 0)
+            go_copy(1, 3, "S")
+            go_mm(1, 0)
+            quant("v1", 1)
+            ga_sum(0, 2)
+            exp_b(1, 2)
+            go_mm(1, 2)
+            go_quant(1, 3, 1)
+            exp_b(1, 0)
+            ga_mm(0, 0)
+            ga_sum(0, 1)
+            exp_b(0, 0)
+            ga_mm(1, 1)
+            make_w(1, 0, "V")
+            exp_b(1, 1)
+            ga_mm(1, 3)
+            make_w(1, 2, "V")
+            go_copy(1, 0, "S")
+            ga_sum(0, 0)
+            go_copy(1, 2, "S")
+            go_quant(1, 0, 1)
+            make_w(0, 0, "V")
             recip_root(1, 0, 0, 384)
-            final(0, 2, 0, 512, "V")
-            recip_sq(1, 2, 0, 384, "S")
-            final(0, 3, 0, 512, "V")
-            store(0, 0, 512)
+            go_quant(1, 2, 1)
+            make_w(1, 1, "V")
+            ga_mm(1, 2)
+            ga_mm(1, 0)
+            ga_sum(1, 1)
+            ga_sum(1, 3)
+            recip_root(1, 1, 384, 128)
+            recip_root(1, 3, 384, 128)
+            ga_sum(1, 0)
+            recip_root(0, 3, 0, 512)
+            ga_sum(1, 2)
+            recip_root(1, 0, 384, 128)
+            recip_root(0, 0, 0, 512)
+            ga_w(1, 0)
             recip_sq(1, 0, 0, 384, "S")
-            final(1, 2, 0, 384, "V")
-            recip_sq(1, 3, 0, 384, "S")
-            final(1, 3, 384, 128, "V")
-            spread(0, 0, 512, "S")
-            final(1, 3, 0, 384, "V")
+            ga_w(0, 0)
+            recip_sq(0, 0, 0, 512, "S")
             final(1, 0, 0, 384, "V")
+            recip_root(0, 2, 0, 512)
+            ga_w(1, 1)
+            recip_sq(1, 1, 384, 128, "S")
+            recip_sq(1, 0, 384, 128, "S")
+            ga_w(0, 2)
+            recip_root(0, 1, 0, 512)
+            ga_w(1, 3)
+            recip_sq(0, 3, 0, 512, "S")
+            ga_w(0, 1)
+            recip_root(1, 3, 0, 384)
+            ga_w(1, 2)
+            recip_sq(0, 1, 0, 512, "S")
+            final(0, 3, 0, 512, "V")
+            recip_root(1, 2, 0, 384)
+            recip_sq(1, 3, 0, 384, "S")
+            final(0, 1, 0, 512, "V")
+            recip_root(1, 1, 0, 384)
+            final(1, 3, 0, 384, "V")
+            recip_sq(0, 2, 0, 512, "S")
+            final(0, 0, 0, 512, "V")
+            recip_sq(1, 1, 0, 384, "S")
+            final(0, 2, 0, 512, "V")
+            store(0, 0, 512)
+            recip_root(1, 2, 384, 128)
+            recip_sq(1, 2, 0, 384, "S")
+            final(1, 1, 0, 384, "V")
+            recip_sq(1, 2, 384, 128, "S")
+            final(1, 2, 0, 384, "V")
             store(1, 0, 384)
-            final(1, 1, 384, 128, "V")
+            recip_sq(1, 3, 384, 128, "S")
+            spread(0, 0, 512, "S")
+            final(1, 3, 384, 128, "V")
             final(1, 2, 384, 128, "V")
-            store(1, 384, 128)
             spread(1, 0, 384, "V")
+            final(1, 1, 384, 128, "V")
+            final(1, 0, 384, 128, "V")
+            store(1, 384, 128)
+            planes(1, 0, 384)
             spread(1, 384, 128, "S")
             planes(0, 0, 512)
-            planes(1, 0, 384)
             planes(1, 384, 128)

@@ -42,6 +42,7 @@ def tile_atpstarsinglekeypatcheffect_x1_kernel(
         nc.vector.memset(warm[:], 0.0)
         nc.scalar.activation(out=warm[:], in_=warm[:], func=ACT.Exp)
 
+        blocked_names = ("k0", "dk0", "v0", "k1", "dk1", "v1")
         raw = {}
         grouped = {}
         codes = {}
@@ -50,13 +51,13 @@ def tile_atpstarsinglekeypatcheffect_x1_kernel(
         def load(name, src, blocked):
             t = keep.tile([P, NT, K], BF16, name="raw_" + name)
             raw[name] = t
-            if blocked:
-                view = src.rearrange("(t p) c -> p t c", p=P)
-            else:
-                view = src.rearrange("(p t) c -> p t c", t=NT)
-            step = 1 if name == "q0" else 2
-            for b in range(0, NT, step):
-                nc.sync.dma_start(out=t[:, b : b + step, :], in_=view[:, b : b + step, :])
+            pieces = [(0, 1), (1, 1), (2, 2)] if name == "q0" else [(0, 2), (2, 2)]
+            for s, n in pieces:
+                if blocked:
+                    view = src[128 * s : 128 * (s + n), :].rearrange("(p e) c -> p e c", e=n)
+                else:
+                    view = src.rearrange("(p t) c -> p t c", t=NT)[:, s : s + n, :]
+                nc.sync.dma_start(out=t[:, s : s + n, :], in_=view)
 
         def dummy():
             bank = new_bank([P, 256])
@@ -75,8 +76,12 @@ def tile_atpstarsinglekeypatcheffect_x1_kernel(
                 g = work.tile([P, S, NT], BF16, name="grouped", align_bytes=64, bufs=10)
                 grouped[name] = g
             dst = grouped[name][:, 256 * b : 256 * b + 256, :].rearrange("p r j -> p (r j)").bitcast(F32)
-            dst = dst.rearrange("p (s r u) -> p s r u", s=2, u=2)
-            src = bank_t[name, b][:].rearrange("p s u r -> p s r u")
+            if name in blocked_names:
+                dst = dst.rearrange("p (r s u) -> p r s u", s=2, u=2)
+                src = bank_t[name, b][:].rearrange("p s u r -> p r s u")
+            else:
+                dst = dst.rearrange("p (s r u) -> p s r u", s=2, u=2)
+                src = bank_t[name, b][:].rearrange("p s u r -> p s r u")
             if eng == "S":
                 nc.scalar.copy(out=dst, in_=src)
             else:
@@ -88,10 +93,11 @@ def tile_atpstarsinglekeypatcheffect_x1_kernel(
                 z = keep.tile([P, S], U8, name="scales_" + name, align_bytes=64)
                 codes[name] = c
                 scales[name] = z
+            cols = slice(0, S) if b < 0 else slice(256 * b, 256 * b + 256)
             nc.vector.quantize_mx(
-                out=codes[name][:, 256 * b : 256 * b + 256].bitcast(FP8X4),
-                scales=scales[name][:, 256 * b : 256 * b + 256],
-                in_=grouped[name][:, 256 * b : 256 * b + 256, :].rearrange("p r j -> p (r j)"),
+                out=codes[name][:, cols].bitcast(FP8X4),
+                scales=scales[name][:, cols],
+                in_=grouped[name][:, cols, :].rearrange("p r j -> p (r j)"),
             )
 
         def mm(dst, a, acols, b, bcols):
@@ -109,7 +115,7 @@ def tile_atpstarsinglekeypatcheffect_x1_kernel(
             return slice(P * c, P * c + P)
 
         ALLC = slice(0, S)
-        zsum, rz, e_t, w_t, gw_t, bank_t, bank_s, bank_d, bank_go, nm_t, big_t, bank_ga, gb_t, r_t, ars_t, out_t, mode, zs = ({} for i in range(18))
+        zsum, rz, e_t, w_t, gw_t, bank_t, bank_s, bank_d, bank_go, nm_t, big_t, bank_ga, gb_t, r_t, ars_t, out_t, mode, zs, done = ({} for i in range(19))
 
         def scores(h, t):
             bank = new_bank([P, S])
@@ -254,10 +260,10 @@ def tile_atpstarsinglekeypatcheffect_x1_kernel(
             e = nc.gpsimd if eng == "G" else nc.vector
             e.tensor_tensor(out=o[:, t, :], in0=gw_t[h, t][:, lo : lo + n], in1=r_t[h, t, lo][:, :n], op=ALU.mult)
 
-        def store(h, lo, n):
-            nc.sync.dma_start(
-                out=out_0[h].rearrange("(p t) j -> p t j", t=NT)[:, :, lo : lo + n], in_=out_t[h, lo][:]
-            )
+        def store(h, lo, n, t):
+            view = out_0[h].rearrange("(p t) j -> p t j", t=NT)
+            rows = slice(t, t + 1) if t >= 0 else slice(0, NT)
+            nc.sync.dma_start(out=view[:, rows, lo : lo + n], in_=out_t[h, lo][:, rows, :])
 
         def spread(h, lo, n, eng):
             if ("out%d" % h) not in codes:
@@ -294,7 +300,8 @@ def tile_atpstarsinglekeypatcheffect_x1_kernel(
             nc.sync.dma_start(
                 out=out_1[0][:, ocols, :].rearrange("p m t -> p (m t)").bitcast(I32), in_=c[:, cols].bitcast(I32)
             )
-            if lo + n == S:
+            done[h] = done.get(h, 0) + n
+            if done[h] == S:
                 cols = slice(S * h, S * h + S)
                 for qd in range(4):
                     q_ = nc.scalar if (h == 1 and qd % 2) else nc.sync
@@ -308,220 +315,217 @@ def tile_atpstarsinglekeypatcheffect_x1_kernel(
                 "dk1": (dk[1], True), "wo1": (wo[1], False), "v1": (v[1], True)}
 
         with tc.manual_schedule():
-            for name in ("q0", "k0", "dk0", "gres", "wo0", "v0", "q1", "k1", "dk1", "wo1", "v1"):
+            for name in ("q0", "k0", "dk0", "gres", "wo0", "q1", "k1", "v0", "dk1", "wo1", "v1"):
                 load(name, *srcs[name])
             dummy()
             dummy()
             turn("q0", 0)
-            dummy()
-            evac("q0", 0, "S")
             turn("q0", 1)
-            turn("k0", 0)
-            evac("q0", 1, "V")
-            turn("k0", 1)
-            evac("k0", 0, "S")
-            quant("q0", 1)
             dummy()
+            evac("q0", 1, "S")
+            turn("k0", 0)
+            evac("q0", 0, "S")
+            turn("k0", 1)
+            evac("k0", 0, "V")
+            turn("dk0", 0)
             evac("k0", 1, "S")
             quant("q0", 0)
-            turn("dk0", 0)
+            dummy()
+            quant("k0", 0)
             quant("k0", 1)
             turn("dk0", 1)
-            quant("k0", 0)
-            evac("dk0", 0, "S")
-            turn("gres", 1)
-            evac("dk0", 1, "S")
+            quant("q0", 1)
+            evac("dk0", 0, "V")
             turn("gres", 0)
-            evac("gres", 1, "S")
-            dummy()
-            evac("gres", 0, "S")
-            quant("gres", 1)
-            quant("dk0", 0)
-            quant("gres", 0)
-            turn("wo0", 0)
-            quant("dk0", 1)
-            turn("wo0", 1)
-            evac("wo0", 0, "S")
-            scores(0, 3)
-            evac("wo0", 1, "S")
-            quant("wo0", 0)
-            scores(0, 1)
-            rowmax(0, 3)
-            scores(0, 2)
+            evac("dk0", 1, "S")
             scores(0, 0)
-            rowmax(0, 1)
-            turn("q1", 0)
+            evac("gres", 0, "S")
+            quant("dk0", -1)
+            scores(0, 3)
+            turn("gres", 1)
+            rowmax(0, 3)
+            turn("wo0", 0)
+            evac("gres", 1, "V")
             exp_s(0, 3)
+            scores(0, 2)
+            rowmax(0, 0)
+            shift(0, 1, "V")
+            evac("wo0", 0, "S")
+            shift(0, 3, "V")
             rowmax(0, 2)
+            scores(0, 1)
+            exp_b(0, 3)
+            turn("q1", 0)
+            rowmax(0, 1)
+            exp_s(0, 2)
+            turn("wo0", 1)
+            evac("q1", 0, "V")
+            exp_s(0, 0)
+            dummy()
+            quant("gres", -1)
+            turn("q1", 1)
+            evac("wo0", 1, "S")
+            make_w(0, 3, "V")
+            turn("k1", 0)
+            exp_b(0, 1)
+            quant("wo0", -1)
             turn("k1", 1)
             exp_s(0, 1)
-            rowmax(0, 0)
-            turn("k1", 0)
-            evac("q1", 0, "S")
-            evac("k1", 1, "V")
-            dummy()
-            exp_s(0, 2)
-            evac("k1", 0, "V")
-            turn("q1", 1)
-            exp_s(0, 0)
-            quant("wo0", 1)
-            turn("v0", 0)
-            quant("k1", 0)
-            evac("q1", 1, "S")
-            quant("q1", 0)
-            go_mm(0, 1)
-            quant("k1", 1)
-            turn("dk1", 0)
-            evac("v0", 0, "S")
-            inv_z(0)
-            quant("q1", 1)
-            go_copy(0, 1, "V")
-            shift(0, 2, "V")
-            evac("dk1", 0, "S")
-            scores(1, 3)
-            quant("v0", 0)
-            shift(0, 3, "V")
-            go_quant(0, 1, 1)
-            exp_b(0, 2)
-            rowmax(1, 3)
-            go_mm(0, 2)
-            scores(1, 1)
-            exp_b(0, 3)
-            make_w(0, 2, "V")
-            shift(0, 1, "V")
-            scores(1, 2)
-            go_copy(0, 2, "S")
-            rowmax(1, 1)
-            scores(1, 0)
-            turn("dk1", 1)
-            exp_b(0, 1)
-            quant("dk1", 0)
-            rowmax(1, 0)
-            exp_s(1, 1)
-            turn("wo1", 0)
+            evac("q1", 1, "V")
+            shift(0, 2, "G")
+            evac("k1", 0, "S")
             make_w(0, 1, "V")
-            go_mm(0, 0)
-            evac("dk1", 1, "S")
-            make_w(0, 3, "V")
             go_mm(0, 3)
-            exp_s(1, 0)
-            turn("v0", 1)
-            quant("dk1", 1)
+            evac("k1", 1, "S")
+            go_mm(0, 2)
+            quant("q1", -1)
+            turn("dk1", 0)
+            go_copy(0, 2, "S")
+            quant("k1", -1)
+            turn("dk1", 1)
             go_copy(0, 3, "S")
-            rowmax(1, 2)
+            evac("dk1", 0, "V")
+            scores(1, 0)
+            exp_b(0, 2)
+            go_mm(0, 1)
+            go_quant(0, 2, 2)
+            scores(1, 3)
+            evac("dk1", 1, "S")
+            rowmax(1, 0)
+            scores(1, 1)
+            go_mm(0, 0)
+            go_copy(0, 1, "S")
+            rowmax(1, 3)
+            make_w(0, 2, "G")
             turn("wo1", 1)
-            evac("wo1", 0, "S")
-            evac("v0", 1, "V")
-            shift(1, 2, "V")
-            shift(1, 0, "V")
-            evac("wo1", 1, "S")
-            go_quant(0, 3, 1)
-            go_quant(0, 2, 1)
-            shift(1, 3, "V")
-            quant("v0", 1)
-            turn("v1", 0)
-            exp_s(1, 2)
+            exp_s(1, 0)
+            rowmax(1, 1)
+            turn("wo1", 0)
             go_copy(0, 0, "V")
-            ga_mm(0, 3)
-            quant("wo1", 0)
-            exp_b(1, 3)
-            quant("wo1", 1)
-            shift(1, 1, "V")
+            evac("wo1", 1, "S")
+            shift(0, 0, "G")
+            quant("dk1", -1)
+            evac("wo1", 0, "S")
+            scores(1, 2)
+            inv_z(0)
             exp_s(1, 3)
-            go_quant(0, 0, 1)
-            go_mm(1, 3)
-            ga_sum(0, 3)
-            go_mm(1, 1)
-            evac("v1", 0, "S")
             turn("v1", 1)
-            inv_z(1)
-            make_w(1, 3, "V")
-            go_copy(1, 1, "S")
-            shift(0, 0, "V")
-            ga_w(0, 3)
-            evac("v1", 1, "S")
-            ga_mm(0, 1)
-            go_quant(1, 1, 1)
-            ga_mm(0, 2)
-            quant("v1", 0)
-            go_copy(1, 3, "S")
+            quant("wo1", -1)
+            exp_s(1, 1)
+            shift(1, 2, "V")
+            rowmax(1, 2)
             go_mm(1, 0)
-            quant("v1", 1)
-            ga_sum(0, 2)
-            exp_b(1, 2)
-            go_mm(1, 2)
-            go_quant(1, 3, 1)
-            exp_b(1, 0)
-            ga_mm(0, 0)
-            ga_sum(0, 1)
+            go_quant(0, 0, 2)
             exp_b(0, 0)
-            ga_mm(1, 1)
-            make_w(1, 0, "V")
-            exp_b(1, 1)
-            ga_mm(1, 3)
+            turn("v0", 0)
+            evac("v1", 1, "V")
+            exp_s(1, 2)
+            make_w(0, 0, "G")
+            turn("v0", 1)
+            go_copy(1, 0, "V")
+            exp_b(1, 2)
+            go_mm(1, 3)
+            evac("v0", 0, "V")
+            go_mm(1, 1)
+            evac("v0", 1, "S")
+            shift(1, 3, "G")
+            inv_z(1)
             make_w(1, 2, "V")
-            go_copy(1, 0, "S")
-            ga_sum(0, 0)
+            go_copy(1, 1, "S")
+            go_mm(1, 2)
+            quant("v0", -1)
+            turn("v1", 0)
+            exp_b(1, 3)
+            go_quant(1, 0, 2)
+            ga_mm(0, 3)
             go_copy(1, 2, "S")
-            go_quant(1, 0, 1)
-            make_w(0, 0, "V")
-            recip_root(1, 0, 0, 384)
-            go_quant(1, 2, 1)
-            make_w(1, 1, "V")
-            ga_mm(1, 2)
-            ga_mm(1, 0)
-            ga_sum(1, 1)
-            ga_sum(1, 3)
-            recip_root(1, 1, 384, 128)
-            recip_root(1, 3, 384, 128)
-            ga_sum(1, 0)
+            make_w(1, 3, "G")
+            evac("v1", 0, "V")
+            shift(1, 0, "G")
+            go_copy(1, 3, "S")
+            ga_sum(0, 3)
+            shift(1, 1, "G")
+            exp_b(1, 0)
+            go_quant(1, 2, 2)
+            ga_mm(0, 2)
+            quant("v1", -1)
+            exp_b(1, 1)
+            ga_mm(0, 1)
+            dummy()
             recip_root(0, 3, 0, 512)
+            ga_sum(0, 2)
+            make_w(1, 1, "G")
+            ga_mm(1, 3)
+            ga_sum(0, 1)
+            ga_mm(1, 2)
+            dummy()
+            make_w(1, 0, "G")
+            ga_w(0, 3)
+            ga_mm(1, 0)
+            ga_sum(1, 3)
+            ga_mm(0, 0)
+            recip_root(1, 2, 0, 256)
+            ga_mm(1, 1)
             ga_sum(1, 2)
-            recip_root(1, 0, 384, 128)
-            recip_root(0, 0, 0, 512)
-            ga_w(1, 0)
-            recip_sq(1, 0, 0, 384, "S")
-            ga_w(0, 0)
-            recip_sq(0, 0, 0, 512, "S")
-            final(1, 0, 0, 384, "V")
+            recip_sq(0, 3, 0, 512, "G")
+            recip_root(1, 1, 0, 256)
+            recip_root(1, 3, 256, 256)
+            ga_sum(0, 0)
+            recip_root(1, 2, 256, 256)
             recip_root(0, 2, 0, 512)
-            ga_w(1, 1)
-            recip_sq(1, 1, 384, 128, "S")
-            recip_sq(1, 0, 384, 128, "S")
             ga_w(0, 2)
-            recip_root(0, 1, 0, 512)
-            ga_w(1, 3)
-            recip_sq(0, 3, 0, 512, "S")
-            ga_w(0, 1)
-            recip_root(1, 3, 0, 384)
+            final(0, 3, 0, 512, "G")
+            store(0, 0, 512, 3)
+            recip_sq(1, 3, 256, 256, "S")
             ga_w(1, 2)
-            recip_sq(0, 1, 0, 512, "S")
-            final(0, 3, 0, 512, "V")
-            recip_root(1, 2, 0, 384)
-            recip_sq(1, 3, 0, 384, "S")
-            final(0, 1, 0, 512, "V")
-            recip_root(1, 1, 0, 384)
-            final(1, 3, 0, 384, "V")
+            recip_sq(1, 2, 0, 256, "S")
             recip_sq(0, 2, 0, 512, "S")
+            ga_sum(1, 1)
+            final(1, 2, 0, 256, "G")
+            store(1, 0, 256, 2)
+            recip_sq(1, 2, 256, 256, "S")
+            ga_sum(1, 0)
+            recip_root(1, 3, 0, 256)
+            final(0, 2, 0, 512, "G")
+            store(0, 0, 512, 2)
+            recip_root(1, 0, 256, 256)
+            ga_w(1, 3)
+            recip_root(0, 0, 0, 512)
+            ga_w(0, 1)
+            final(1, 2, 256, 256, "G")
+            store(1, 256, 256, 2)
+            recip_sq(1, 1, 0, 256, "S")
+            recip_root(0, 1, 0, 512)
+            ga_w(1, 1)
+            final(1, 3, 256, 256, "G")
+            store(1, 256, 256, 3)
+            ga_w(0, 0)
+            recip_root(1, 1, 256, 256)
+            recip_sq(0, 0, 0, 512, "S")
+            final(1, 1, 0, 256, "G")
+            store(1, 0, 256, 1)
+            ga_w(1, 0)
+            recip_sq(1, 1, 256, 256, "S")
             final(0, 0, 0, 512, "V")
-            recip_sq(1, 1, 0, 384, "S")
-            final(0, 2, 0, 512, "V")
-            store(0, 0, 512)
-            recip_root(1, 2, 384, 128)
-            recip_sq(1, 2, 0, 384, "S")
-            final(1, 1, 0, 384, "V")
-            recip_sq(1, 2, 384, 128, "S")
-            final(1, 2, 0, 384, "V")
-            store(1, 0, 384)
-            recip_sq(1, 3, 384, 128, "S")
-            spread(0, 0, 512, "S")
-            final(1, 3, 384, 128, "V")
-            final(1, 2, 384, 128, "V")
-            spread(1, 0, 384, "V")
-            final(1, 1, 384, 128, "V")
-            final(1, 0, 384, 128, "V")
-            store(1, 384, 128)
-            planes(1, 0, 384)
-            spread(1, 384, 128, "S")
+            store(0, 0, 512, 0)
+            recip_sq(0, 1, 0, 512, "S")
+            final(1, 1, 256, 256, "V")
+            store(1, 256, 256, 1)
+            recip_root(1, 0, 0, 256)
+            final(0, 1, 0, 512, "V")
+            store(0, 0, 512, 1)
+            recip_sq(1, 0, 256, 256, "S")
+            recip_sq(1, 0, 0, 256, "S")
+            final(1, 0, 256, 256, "V")
+            store(1, 256, 256, 0)
+            recip_sq(1, 3, 0, 256, "S")
+            final(1, 0, 0, 256, "V")
+            store(1, 0, 256, 0)
+            spread(1, 256, 256, "S")
+            final(1, 3, 0, 256, "V")
+            store(1, 0, 256, 3)
+            spread(0, 0, 512, "V")
+            spread(1, 0, 256, "S")
+            planes(1, 256, 256)
             planes(0, 0, 512)
-            planes(1, 384, 128)
+            planes(1, 0, 256)

@@ -236,7 +236,7 @@ def tile_atpstarsinglekeypatcheffect_x1_kernel(
             )
 
         def recip_root(h, t, lo, n):
-            a = work.tile([P, S], F32, name="ars", bufs=6)
+            a = keep.tile([P, n], F32, name="ars%d_%d_%d" % (h, t, lo))
             ars_t[h, t, lo] = a
             nc.scalar.activation(
                 out=a[:, :n], in_=w_t[h, t][:, lo : lo + n], func=ACT.Abs_reciprocal_sqrt,
@@ -244,21 +244,21 @@ def tile_atpstarsinglekeypatcheffect_x1_kernel(
             )
 
         def recip_sq(h, t, lo, n, eng):
-            r = work.tile([P, S], F32, name="r", bufs=6)
-            r_t[h, t, lo] = r
             a = ars_t[h, t, lo]
+            r = a
+            r_t[h, t, lo] = r
             if eng == "G":
                 nc.gpsimd.tensor_tensor(out=r[:, :n], in0=a[:, :n], in1=a[:, :n], op=ALU.mult)
             else:
                 nc.scalar.activation(out=r[:, :n], in_=a[:, :n], func=ACT.Square)
 
-        def final(h, t, lo, n, eng):
+        def final(h, t, lo, n, eng, base):
             if (h, lo) not in out_t:
                 o = keep.tile([P, NT, n], F32, name="out%d_%d" % (h, lo))
                 out_t[h, lo] = o
             o = out_t[h, lo]
             e = nc.gpsimd if eng == "G" else nc.vector
-            e.tensor_tensor(out=o[:, t, :], in0=gw_t[h, t][:, lo : lo + n], in1=r_t[h, t, lo][:, :n], op=ALU.mult)
+            e.tensor_tensor(out=o[:, t, :], in0=gw_t[h, t][:, lo : lo + n], in1=r_t[h, t, base][:, lo - base : lo - base + n], op=ALU.mult)
 
         def store(h, lo, n, t):
             view = out_0[h].rearrange("(p t) j -> p t j", t=NT)
@@ -321,211 +321,214 @@ def tile_atpstarsinglekeypatcheffect_x1_kernel(
             dummy()
             turn("q0", 0)
             turn("q0", 1)
+            evac("q0", 0, "S")
             dummy()
             evac("q0", 1, "S")
-            turn("k0", 0)
-            evac("q0", 0, "S")
-            turn("k0", 1)
-            evac("k0", 0, "V")
-            turn("dk0", 0)
-            evac("k0", 1, "S")
             quant("q0", 0)
-            dummy()
-            quant("k0", 0)
-            quant("k0", 1)
-            turn("dk0", 1)
+            turn("k0", 1)
             quant("q0", 1)
-            evac("dk0", 0, "V")
-            turn("gres", 0)
-            evac("dk0", 1, "S")
-            scores(0, 0)
-            evac("gres", 0, "S")
-            quant("dk0", -1)
-            scores(0, 3)
+            turn("k0", 0)
+            evac("k0", 1, "V")
+            turn("dk0", 0)
+            evac("k0", 0, "S")
+            quant("k0", 1)
+            dummy()
+            evac("dk0", 0, "S")
+            quant("k0", 0)
+            turn("dk0", 1)
             turn("gres", 1)
-            rowmax(0, 3)
-            turn("wo0", 0)
-            evac("gres", 1, "V")
-            exp_s(0, 3)
-            scores(0, 2)
+            evac("dk0", 1, "V")
+            scores(0, 0)
+            evac("gres", 1, "S")
+            scores(0, 3)
             rowmax(0, 0)
-            shift(0, 1, "V")
-            evac("wo0", 0, "S")
-            shift(0, 3, "V")
-            rowmax(0, 2)
             scores(0, 1)
-            exp_b(0, 3)
-            turn("q1", 0)
+            scores(0, 2)
             rowmax(0, 1)
-            exp_s(0, 2)
-            turn("wo0", 1)
-            evac("q1", 0, "V")
+            turn("q1", 0)
             exp_s(0, 0)
-            dummy()
-            quant("gres", -1)
+            rowmax(0, 2)
             turn("q1", 1)
-            evac("wo0", 1, "S")
-            make_w(0, 3, "V")
-            turn("k1", 0)
-            exp_b(0, 1)
-            quant("wo0", -1)
-            turn("k1", 1)
             exp_s(0, 1)
-            evac("q1", 1, "V")
-            shift(0, 2, "G")
-            evac("k1", 0, "S")
-            make_w(0, 1, "V")
-            go_mm(0, 3)
+            rowmax(0, 3)
+            dummy()
+            evac("q1", 1, "S")
+            evac("q1", 0, "V")
+            turn("k1", 1)
+            exp_s(0, 2)
+            quant("dk0", -1)
+            turn("k1", 0)
+            turn("gres", 0)
             evac("k1", 1, "S")
-            go_mm(0, 2)
             quant("q1", -1)
-            turn("dk1", 0)
-            go_copy(0, 2, "S")
+            dummy()
+            evac("k1", 0, "S")
+            evac("gres", 0, "V")
+            turn("wo0", 0)
+            exp_s(0, 3)
             quant("k1", -1)
-            turn("dk1", 1)
-            go_copy(0, 3, "S")
-            evac("dk1", 0, "V")
-            scores(1, 0)
-            exp_b(0, 2)
-            go_mm(0, 1)
-            go_quant(0, 2, 2)
-            scores(1, 3)
-            evac("dk1", 1, "S")
-            rowmax(1, 0)
-            scores(1, 1)
-            go_mm(0, 0)
-            go_copy(0, 1, "S")
-            rowmax(1, 3)
-            make_w(0, 2, "G")
-            turn("wo1", 1)
-            exp_s(1, 0)
-            rowmax(1, 1)
-            turn("wo1", 0)
-            go_copy(0, 0, "V")
-            evac("wo1", 1, "S")
-            shift(0, 0, "G")
-            quant("dk1", -1)
-            evac("wo1", 0, "S")
-            scores(1, 2)
+            turn("wo0", 1)
+            evac("wo0", 0, "S")
             inv_z(0)
-            exp_s(1, 3)
-            turn("v1", 1)
-            quant("wo1", -1)
-            exp_s(1, 1)
-            shift(1, 2, "V")
-            rowmax(1, 2)
-            go_mm(1, 0)
-            go_quant(0, 0, 2)
+            quant("gres", -1)
+            shift(0, 2, "V")
+            evac("wo0", 1, "S")
+            scores(1, 0)
+            shift(0, 0, "V")
+            exp_b(0, 2)
+            rowmax(1, 0)
+            scores(1, 3)
+            shift(0, 1, "V")
             exp_b(0, 0)
-            turn("v0", 0)
-            evac("v1", 1, "V")
+            quant("wo0", -1)
+            shift(0, 3, "G")
+            exp_b(0, 1)
+            scores(1, 1)
+            rowmax(1, 3)
+            scores(1, 2)
+            exp_s(1, 0)
+            turn("dk1", 0)
+            rowmax(1, 1)
+            exp_b(0, 3)
+            rowmax(1, 2)
+            turn("dk1", 1)
+            make_w(0, 1, "V")
+            go_mm(0, 0)
+            exp_s(1, 1)
+            go_mm(0, 3)
+            evac("dk1", 0, "V")
+            make_w(0, 3, "G")
+            evac("dk1", 1, "S")
+            turn("wo1", 1)
+            go_copy(0, 0, "V")
             exp_s(1, 2)
-            make_w(0, 0, "G")
+            turn("wo1", 0)
+            go_copy(0, 3, "V")
+            evac("wo1", 1, "S")
+            go_mm(0, 2)
+            quant("dk1", -1)
+            go_mm(0, 1)
+            evac("wo1", 0, "S")
             turn("v0", 1)
-            go_copy(1, 0, "V")
-            exp_b(1, 2)
+            make_w(0, 0, "V")
+            go_copy(0, 2, "S")
+            turn("v0", 0)
+            quant("wo1", -1)
+            go_copy(0, 1, "S")
+            shift(1, 2, "G")
+            make_w(0, 2, "V")
+            exp_s(1, 3)
             go_mm(1, 3)
-            evac("v0", 0, "V")
-            go_mm(1, 1)
-            evac("v0", 1, "S")
-            shift(1, 3, "G")
-            inv_z(1)
-            make_w(1, 2, "V")
-            go_copy(1, 1, "S")
+            go_quant(0, 2, 2)
+            go_mm(1, 0)
+            exp_b(1, 2)
+            go_quant(0, 0, 2)
             go_mm(1, 2)
-            quant("v0", -1)
+            evac("v0", 0, "V")
+            evac("v0", 1, "S")
             turn("v1", 0)
-            exp_b(1, 3)
-            go_quant(1, 0, 2)
-            ga_mm(0, 3)
-            go_copy(1, 2, "S")
-            make_w(1, 3, "G")
-            evac("v1", 0, "V")
-            shift(1, 0, "G")
+            make_w(1, 2, "G")
+            go_copy(1, 0, "V")
             go_copy(1, 3, "S")
-            ga_sum(0, 3)
-            shift(1, 1, "G")
-            exp_b(1, 0)
+            turn("v1", 1)
+            evac("v1", 0, "V")
+            go_copy(1, 2, "S")
+            go_mm(1, 1)
+            shift(1, 3, "G")
+            quant("v0", -1)
+            evac("v1", 1, "S")
+            shift(1, 0, "G")
             go_quant(1, 2, 2)
-            ga_mm(0, 2)
+            go_copy(1, 1, "S")
             quant("v1", -1)
-            exp_b(1, 1)
             ga_mm(0, 1)
-            dummy()
-            recip_root(0, 3, 0, 512)
-            ga_sum(0, 2)
-            make_w(1, 1, "G")
-            ga_mm(1, 3)
-            ga_sum(0, 1)
+            exp_b(1, 3)
+            shift(1, 1, "G")
+            go_quant(1, 0, 2)
+            exp_b(1, 0)
+            inv_z(1)
+            make_w(1, 3, "G")
             ga_mm(1, 2)
-            dummy()
-            make_w(1, 0, "G")
-            ga_w(0, 3)
+            ga_sum(0, 1)
+            ga_mm(0, 3)
+            exp_b(1, 1)
             ga_mm(1, 0)
-            ga_sum(1, 3)
-            ga_mm(0, 0)
-            recip_root(1, 2, 0, 256)
-            ga_mm(1, 1)
             ga_sum(1, 2)
-            recip_sq(0, 3, 0, 512, "G")
-            recip_root(1, 1, 0, 256)
-            recip_root(1, 3, 256, 256)
-            ga_sum(0, 0)
-            recip_root(1, 2, 256, 256)
-            recip_root(0, 2, 0, 512)
-            ga_w(0, 2)
-            final(0, 3, 0, 512, "G")
-            store(0, 0, 512, 3)
-            recip_sq(1, 3, 256, 256, "S")
-            ga_w(1, 2)
-            recip_sq(1, 2, 0, 256, "S")
-            recip_sq(0, 2, 0, 512, "S")
-            ga_sum(1, 1)
-            final(1, 2, 0, 256, "G")
-            store(1, 0, 256, 2)
-            recip_sq(1, 2, 256, 256, "S")
-            ga_sum(1, 0)
-            recip_root(1, 3, 0, 256)
-            final(0, 2, 0, 512, "G")
-            store(0, 0, 512, 2)
-            recip_root(1, 0, 256, 256)
-            ga_w(1, 3)
-            recip_root(0, 0, 0, 512)
-            ga_w(0, 1)
-            final(1, 2, 256, 256, "G")
-            store(1, 256, 256, 2)
-            recip_sq(1, 1, 0, 256, "S")
+            ga_mm(1, 1)
             recip_root(0, 1, 0, 512)
-            ga_w(1, 1)
-            final(1, 3, 256, 256, "G")
-            store(1, 256, 256, 3)
-            ga_w(0, 0)
+            ga_mm(0, 2)
+            make_w(1, 0, "G")
+            ga_w(0, 1)
+            ga_mm(1, 3)
+            ga_mm(0, 0)
+            ga_sum(0, 3)
+            make_w(1, 1, "G")
+            ga_sum(1, 3)
+            ga_w(0, 3)
+            recip_root(0, 3, 0, 512)
+            recip_sq(0, 1, 0, 512, "G")
+            ga_sum(1, 0)
+            recip_root(1, 0, 256, 256)
+            recip_sq(0, 3, 0, 512, "S")
+            ga_w(1, 3)
+            recip_root(1, 2, 256, 256)
+            final(0, 3, 0, 512, "G", 0)
+            store(0, 0, 512, 3)
+            ga_sum(1, 1)
             recip_root(1, 1, 256, 256)
-            recip_sq(0, 0, 0, 512, "S")
-            final(1, 1, 0, 256, "G")
-            store(1, 0, 256, 1)
-            ga_w(1, 0)
-            recip_sq(1, 1, 256, 256, "S")
-            final(0, 0, 0, 512, "V")
-            store(0, 0, 512, 0)
-            recip_sq(0, 1, 0, 512, "S")
-            final(1, 1, 256, 256, "V")
-            store(1, 256, 256, 1)
-            recip_root(1, 0, 0, 256)
-            final(0, 1, 0, 512, "V")
-            store(0, 0, 512, 1)
             recip_sq(1, 0, 256, 256, "S")
-            recip_sq(1, 0, 0, 256, "S")
-            final(1, 0, 256, 256, "V")
-            store(1, 256, 256, 0)
+            ga_sum(0, 0)
+            recip_root(0, 0, 0, 512)
+            final(0, 1, 0, 512, "G", 0)
+            store(0, 0, 512, 1)
+            ga_w(1, 2)
+            recip_sq(1, 1, 256, 256, "S")
+            recip_sq(1, 2, 256, 256, "S")
+            ga_w(0, 0)
+            recip_sq(0, 0, 0, 512, "S")
+            final(1, 2, 256, 128, "G", 256)
+            ga_w(1, 1)
+            recip_root(1, 2, 0, 256)
+            final(0, 0, 0, 512, "G", 0)
+            store(0, 0, 512, 0)
+            recip_root(1, 3, 256, 256)
+            ga_sum(0, 2)
+            recip_root(1, 3, 0, 256)
+            ga_w(1, 0)
+            recip_sq(1, 2, 0, 256, "S")
+            recip_sq(1, 3, 256, 256, "S")
+            final(1, 1, 256, 128, "G", 256)
+            ga_w(0, 2)
             recip_sq(1, 3, 0, 256, "S")
-            final(1, 0, 0, 256, "V")
-            store(1, 0, 256, 0)
-            spread(1, 256, 256, "S")
-            final(1, 3, 0, 256, "V")
+            final(1, 2, 384, 128, "G", 256)
+            recip_root(0, 2, 0, 512)
+            final(1, 3, 0, 256, "V", 0)
             store(1, 0, 256, 3)
+            final(1, 2, 0, 256, "V", 0)
+            store(1, 0, 256, 2)
+            recip_root(1, 0, 0, 256)
+            final(1, 0, 384, 128, "V", 256)
+            recip_sq(0, 2, 0, 512, "S")
+            final(1, 1, 384, 128, "V", 256)
+            final(1, 3, 384, 128, "V", 256)
+            store(1, 384, 128, -1)
+            final(1, 0, 256, 128, "V", 256)
+            final(1, 3, 256, 128, "V", 256)
+            store(1, 256, 128, -1)
+            recip_root(1, 1, 0, 256)
+            final(0, 2, 0, 512, "V", 0)
+            store(0, 0, 512, 2)
+            recip_sq(1, 0, 0, 256, "S")
+            recip_sq(1, 1, 0, 256, "S")
+            final(1, 0, 0, 256, "V", 0)
+            store(1, 0, 256, 0)
+            spread(1, 256, 128, "S")
+            final(1, 1, 0, 256, "V", 0)
+            store(1, 0, 256, 1)
             spread(0, 0, 512, "V")
+            spread(1, 384, 128, "S")
             spread(1, 0, 256, "S")
-            planes(1, 256, 256)
+            planes(1, 256, 128)
+            planes(1, 384, 128)
             planes(0, 0, 512)
             planes(1, 0, 256)

from contextlib import ExitStack

import concourse.mybir as mybir
from concourse.masks import make_identity

HEADS, S, K = 2, 512, 512
P = 128
NT = 4
SCALE = 1.0 / (512.0 ** 0.5)

F32 = mybir.dt.float32
BF16 = mybir.dt.bfloat16
U32 = mybir.dt.uint32
I32 = mybir.dt.int32
U8 = mybir.dt.uint8
FP8X4 = mybir.dt.float8_e4m3fn_x4
ALU = mybir.AluOpType
ACT = mybir.ActivationFunctionType
AX = mybir.AxisListType

FLOPS = 2 * 4 * 2 * S * S * K + 15 * HEADS * S * S


def tile_atpstarsinglekeypatcheffect_x1_kernel(
    tc, q, k, dk, v, gres, wo, out_0, out_1, out_2
):
    nc = tc.nc
    with ExitStack() as ctx:
        keep = ctx.enter_context(tc.tile_pool(name="keep", bufs=1))
        work = ctx.enter_context(tc.tile_pool(name="work", bufs=4))
        psum = ctx.enter_context(tc.psum_pool(name="psum", bufs=8))

        def new_bank(shape):
            bank = psum.tile(shape, F32, name="bank")
            return bank

        ident = keep.tile([P, P], F32, name="ident")
        make_identity(nc, ident[:])
        zero = keep.tile([P, 256], F32, name="zero")
        nc.vector.memset(zero[:], 0.0)
        warm = keep.tile([P, 1], F32, name="warm")
        nc.vector.memset(warm[:], 0.0)
        nc.scalar.activation(out=warm[:], in_=warm[:], func=ACT.Exp)

        blocked_names = ("k0", "dk0", "v0", "k1", "dk1", "v1")
        raw = {}
        grouped = {}
        codes = {}
        scales = {}

        def load(name, src, blocked):
            t = keep.tile([P, NT, K], BF16, name="raw_" + name)
            raw[name] = t
            pieces = [(0, 1), (1, 1), (2, 2)] if name == "q0" else [(0, 2), (2, 2)]
            for s, n in pieces:
                if blocked:
                    view = src[128 * s : 128 * (s + n), :].rearrange("(p e) c -> p e c", e=n)
                else:
                    view = src.rearrange("(p t) c -> p t c", t=NT)[:, s : s + n, :]
                nc.sync.dma_start(out=t[:, s : s + n, :], in_=view)

        def dummy():
            bank = new_bank([P, 256])
            nc.tensor.matmul(bank[:], lhsT=zero[:, :P], rhs=zero[:], start=True, stop=True)

        def turn(name, b):
            bank = new_bank([P, 2, 2, P])
            bank_t[name, b] = bank
            for s in range(2):
                words = raw[name][:, 2 * b + s, :].bitcast(F32)
                for u in range(2):
                    nc.tensor.transpose(bank[:, s, u, :], words[:, u : 2 * P : 2], ident[:])

        def evac(name, b, eng):
            if name not in grouped:
                g = work.tile([P, S, NT], BF16, name="grouped", align_bytes=64, bufs=10)
                grouped[name] = g
            dst = grouped[name][:, 256 * b : 256 * b + 256, :].rearrange("p r j -> p (r j)").bitcast(F32)
            if name in blocked_names:
                dst = dst.rearrange("p (r s u) -> p r s u", s=2, u=2)
                src = bank_t[name, b][:].rearrange("p s u r -> p r s u")
            else:
                dst = dst.rearrange("p (s r u) -> p s r u", s=2, u=2)
                src = bank_t[name, b][:].rearrange("p s u r -> p s r u")
            if eng == "S":
                nc.scalar.copy(out=dst, in_=src)
            else:
                nc.vector.tensor_copy(out=dst, in_=src)

        def quant(name, b):
            if name not in codes:
                c = keep.tile([P, S], U32, name="codes_" + name, align_bytes=64)
                z = keep.tile([P, S], U8, name="scales_" + name, align_bytes=64)
                codes[name] = c
                scales[name] = z
            cols = slice(0, S) if b < 0 else slice(256 * b, 256 * b + 256)
            nc.vector.quantize_mx(
                out=codes[name][:, cols].bitcast(FP8X4),
                scales=scales[name][:, cols],
                in_=grouped[name][:, cols, :].rearrange("p r j -> p (r j)"),
            )

        def mm(dst, a, acols, b, bcols):
            nc.tensor.matmul_mx(
                out=dst,
                lhsT=codes[a][:, acols].bitcast(FP8X4),
                lhsT_scale=scales[a][:, acols],
                rhs=codes[b][:, bcols].bitcast(FP8X4),
                rhs_scale=scales[b][:, bcols],
                start=True,
                stop=True,
            )

        def sl(c):
            return slice(P * c, P * c + P)

        ALLC = slice(0, S)
        zsum, rz, e_t, w_t, gw_t, bank_t, bank_s, bank_d, bank_go, nm_t, big_t, bank_ga, gb_t, r_t, ars_t, out_t, mode, zs, done = ({} for i in range(19))

        def scores(h, t):
            bank = new_bank([P, S])
            bank_s[h, t] = bank
            mm(bank[:], "q%d" % h, sl(t), "k%d" % h, ALLC)

        def rowmax(h, t):
            m = work.tile([P, 1], F32, name="m", bufs=8)
            nc.vector.tensor_reduce(out=m[:], in_=bank_s[h, t][:], axis=AX.X, op=ALU.max)
            nm = work.tile([P, 1], F32, name="nm", bufs=8)
            nm_t[h, t] = nm
            nc.gpsimd.tensor_scalar(out=nm[:], in0=m[:], scalar1=-SCALE, scalar2=0.0, op0=ALU.mult, op1=ALU.add)

        def exp_s(h, t):
            if h not in zsum:
                zz = keep.tile([P, NT], F32, name="zsum%d" % h)
                zsum[h] = zz
            e = keep.tile([P, S], F32, name="e%d" % (4 * h + t))
            e_t[h, t] = e
            nc.scalar.activation(
                out=e[:], in_=bank_s[h, t][:], func=ACT.Exp, bias=nm_t[h, t][:], scale=SCALE,
                accum_out=zsum[h][:, t : t + 1],
            )

        def shift(h, t, eng):
            bank = new_bank([P, S])
            bank_d[h, t] = bank
            mode[h, t] = eng
            names = ["k%d" % h, "dk%d" % h] if eng == "G" else ["dk%d" % h]
            for name in names:
                nc.tensor.matmul_mx(
                    out=bank[:],
                    lhsT=codes["q%d" % h][:, sl(t)].bitcast(FP8X4),
                    lhsT_scale=scales["q%d" % h][:, sl(t)],
                    rhs=codes[name][:].bitcast(FP8X4),
                    rhs_scale=scales[name][:],
                    start=(name == names[0]),
                    stop=(name == names[-1]),
                )

        def exp_b(h, t):
            big = keep.tile([P, S], F32, name="big%d" % (4 * h + t))
            big_t[h, t] = big
            if mode[h, t] == "G":
                nc.scalar.activation(out=big[:], in_=bank_d[h, t][:], func=ACT.Exp, bias=nm_t[h, t][:], scale=SCALE)
            else:
                nc.scalar.activation(out=big[:], in_=bank_d[h, t][:], func=ACT.Exp, scale=SCALE)

        def make_w(h, t, eng):
            w = keep.tile([P, S], F32, name="w%d" % (4 * h + t))
            w_t[h, t] = w
            if mode[h, t] == "G":
                e = nc.gpsimd if eng == "G" else nc.vector
                e.tensor_tensor(out=w[:], in0=big_t[h, t][:], in1=e_t[h, t][:], op=ALU.subtract)
            else:
                nc.vector.scalar_tensor_tensor(
                    out=w[:], in0=big_t[h, t][:], scalar=-1.0, in1=e_t[h, t][:], op0=ALU.add, op1=ALU.mult
                )

        def go_mm(h, c):
            if ("go%d" % h) not in codes:
                g = work.tile([P, S, NT], BF16, name="grouped", align_bytes=64, bufs=10)
                grouped["go%d" % h] = g
                cc = keep.tile([P, S], U32, name="codes_go%d" % h, align_bytes=64)
                z = keep.tile([P, S], U8, name="scales_go%d" % h, align_bytes=64)
                codes["go%d" % h] = cc
                scales["go%d" % h] = z
            bank = new_bank([P, NT, P])
            bank_go[h, c] = bank
            for j in range(NT):
                mm(bank[:, j, :], "wo%d" % h, sl(j), "gres", sl(c))

        def go_copy(h, c, eng):
            dst = grouped["go%d" % h][:, sl(c), :]
            src = bank_go[h, c][:].rearrange("p j n -> p n j")
            if eng == "S":
                nc.scalar.copy(out=dst, in_=src)
            else:
                nc.vector.tensor_copy(out=dst, in_=src)

        def go_quant(h, c, n):
            cols = slice(P * c, P * (c + n))
            nc.vector.quantize_mx(
                out=codes["go%d" % h][:, cols].bitcast(FP8X4),
                scales=scales["go%d" % h][:, cols],
                in_=grouped["go%d" % h][:, cols, :].rearrange("p r j -> p (r j)"),
            )

        def inv_z(h):
            r = keep.tile([P, NT], F32, name="rz%d" % h)
            rz[h] = r
            nc.vector.reciprocal(r[:], zsum[h][:])
            zz = keep.tile([P, NT], F32, name="zs%d" % h)
            zs[h] = zz
            nc.vector.tensor_scalar(out=zz[:], in0=zsum[h][:], scalar1=1.0 / 512.0, scalar2=None, op0=ALU.mult)

        def ga_mm(h, t):
            bank = new_bank([P, S])
            bank_ga[h, t] = bank
            mm(bank[:], "go%d" % h, sl(t), "v%d" % h, ALLC)

        def ga_sum(h, t):
            bank = bank_ga[h, t]
            junk = work.tile([P, S], F32, name="junk", bufs=2)
            gb = work.tile([P, 1], F32, name="gb", bufs=8)
            gb_t[h, t] = gb
            nc.vector.scalar_tensor_tensor(
                out=junk[:], in0=bank[:], scalar=rz[h][:, t : t + 1], in1=e_t[h, t][:],
                op0=ALU.mult, op1=ALU.mult, accum_out=gb[:],
            )

        def ga_w(h, t):
            gw = keep.tile([P, S], F32, name="gw%d" % (4 * h + t))
            gw_t[h, t] = gw
            nc.vector.scalar_tensor_tensor(
                out=gw[:], in0=bank_ga[h, t][:], scalar=gb_t[h, t][:], in1=w_t[h, t][:],
                op0=ALU.subtract, op1=ALU.mult,
            )

        def recip_root(h, t, lo, n):
            a = keep.tile([P, n], F32, name="ars%d_%d_%d" % (h, t, lo))
            ars_t[h, t, lo] = a
            nc.scalar.activation(
                out=a[:, :n], in_=w_t[h, t][:, lo : lo + n], func=ACT.Abs_reciprocal_sqrt,
                bias=zs[h][:, t : t + 1], scale=1.0 / 512.0,
            )

        def recip_sq(h, t, lo, n, eng):
            a = ars_t[h, t, lo]
            r = a
            r_t[h, t, lo] = r
            if eng == "G":
                nc.gpsimd.tensor_tensor(out=r[:, :n], in0=a[:, :n], in1=a[:, :n], op=ALU.mult)
            else:
                nc.scalar.activation(out=r[:, :n], in_=a[:, :n], func=ACT.Square)

        def final(h, t, lo, n, eng, base):
            if (h, lo) not in out_t:
                o = keep.tile([P, NT, n], F32, name="out%d_%d" % (h, lo))
                out_t[h, lo] = o
            o = out_t[h, lo]
            e = nc.gpsimd if eng == "G" else nc.vector
            e.tensor_tensor(out=o[:, t, :], in0=gw_t[h, t][:, lo : lo + n], in1=r_t[h, t, base][:, lo - base : lo - base + n], op=ALU.mult)

        def store(h, lo, n, t):
            view = out_0[h].rearrange("(p t) j -> p t j", t=NT)
            rows = slice(t, t + 1) if t >= 0 else slice(0, NT)
            nc.sync.dma_start(out=view[:, rows, lo : lo + n], in_=out_t[h, lo][:, rows, :])

        def spread(h, lo, n, eng):
            if ("out%d" % h) not in codes:
                g = work.tile([P, S, NT], BF16, name="grouped", align_bytes=64, bufs=10)
                grouped["out%d" % h] = g
                c = keep.tile([P, S], U32, name="ocodes%d" % h, align_bytes=64)
                z = keep.tile([P, S], U8, name="oscales%d" % h, align_bytes=64)
                codes["out%d" % h] = c
                scales["out%d" % h] = z
            dst = grouped["out%d" % h][:, lo : lo + n, :]
            src = out_t[h, lo][:].rearrange("p t j -> p j t")
            if eng == "S":
                nc.scalar.copy(out=dst, in_=src)
            elif eng == "G":
                nc.gpsimd.tensor_scalar(out=dst, in0=src, scalar1=1.0, scalar2=0.0, op0=ALU.mult, op1=ALU.add)
            else:
                nc.vector.tensor_copy(out=dst, in_=src)

        def planes(h, lo, n):
            c, z = codes["out%d" % h], scales["out%d" % h]
            w = 512
            at = lo
            while at < lo + n:
                while w > lo + n - at:
                    w = w // 2
                cols = slice(at, at + w)
                nc.vector.quantize_mx(
                    out=c[:, cols].bitcast(FP8X4), scales=z[:, cols],
                    in_=grouped["out%d" % h][:, cols, :].rearrange("p r j -> p (r j)"),
                )
                at = at + w
            cols = slice(lo, lo + n)
            ocols = slice(S * h + lo, S * h + lo + n)
            nc.sync.dma_start(
                out=out_1[0][:, ocols, :].rearrange("p m t -> p (m t)").bitcast(I32), in_=c[:, cols].bitcast(I32)
            )
            done[h] = done.get(h, 0) + n
            if done[h] == S:
                cols = slice(S * h, S * h + S)
                for qd in range(4):
                    q_ = nc.scalar if (h == 1 and qd % 2) else nc.sync
                    q_.dma_start(
                        out=out_2[0, 4 * qd : 4 * qd + 4, cols].bitcast(I32),
                        in_=z[32 * qd : 32 * qd + 4, :].bitcast(I32),
                    )

        srcs = {"q0": (q[0], False), "k0": (k[0], True), "dk0": (dk[0], True), "gres": (gres, False),
                "wo0": (wo[0], False), "v0": (v[0], True), "q1": (q[1], False), "k1": (k[1], True),
                "dk1": (dk[1], True), "wo1": (wo[1], False), "v1": (v[1], True)}

        with tc.manual_schedule():
            for name in ("q0", "k0", "dk0", "gres", "wo0", "q1", "k1", "v0", "dk1", "wo1", "v1"):
                load(name, *srcs[name])
            dummy()
            dummy()
            turn("q0", 0)
            turn("q0", 1)
            evac("q0", 0, "S")
            dummy()
            evac("q0", 1, "S")
            quant("q0", 0)
            turn("k0", 1)
            quant("q0", 1)
            turn("k0", 0)
            evac("k0", 1, "V")
            turn("dk0", 0)
            evac("k0", 0, "S")
            quant("k0", 1)
            dummy()
            evac("dk0", 0, "S")
            quant("k0", 0)
            turn("dk0", 1)
            turn("gres", 1)
            evac("dk0", 1, "V")
            scores(0, 0)
            evac("gres", 1, "S")
            scores(0, 3)
            rowmax(0, 0)
            scores(0, 1)
            scores(0, 2)
            rowmax(0, 1)
            turn("q1", 0)
            exp_s(0, 0)
            rowmax(0, 2)
            turn("q1", 1)
            exp_s(0, 1)
            rowmax(0, 3)
            dummy()
            evac("q1", 1, "S")
            evac("q1", 0, "V")
            turn("k1", 1)
            exp_s(0, 2)
            quant("dk0", -1)
            turn("k1", 0)
            turn("gres", 0)
            evac("k1", 1, "S")
            quant("q1", -1)
            dummy()
            evac("k1", 0, "S")
            evac("gres", 0, "V")
            turn("wo0", 0)
            exp_s(0, 3)
            quant("k1", -1)
            turn("wo0", 1)
            evac("wo0", 0, "S")
            inv_z(0)
            quant("gres", -1)
            shift(0, 2, "V")
            evac("wo0", 1, "S")
            scores(1, 0)
            shift(0, 0, "V")
            exp_b(0, 2)
            rowmax(1, 0)
            scores(1, 3)
            shift(0, 1, "V")
            exp_b(0, 0)
            quant("wo0", -1)
            shift(0, 3, "G")
            exp_b(0, 1)
            scores(1, 1)
            rowmax(1, 3)
            scores(1, 2)
            exp_s(1, 0)
            turn("dk1", 0)
            rowmax(1, 1)
            exp_b(0, 3)
            rowmax(1, 2)
            turn("dk1", 1)
            make_w(0, 1, "V")
            go_mm(0, 0)
            exp_s(1, 1)
            go_mm(0, 3)
            evac("dk1", 0, "V")
            make_w(0, 3, "G")
            evac("dk1", 1, "S")
            turn("wo1", 1)
            go_copy(0, 0, "V")
            exp_s(1, 2)
            turn("wo1", 0)
            go_copy(0, 3, "V")
            evac("wo1", 1, "S")
            go_mm(0, 2)
            quant("dk1", -1)
            go_mm(0, 1)
            evac("wo1", 0, "S")
            turn("v0", 1)
            make_w(0, 0, "V")
            go_copy(0, 2, "S")
            turn("v0", 0)
            quant("wo1", -1)
            go_copy(0, 1, "S")
            shift(1, 2, "G")
            make_w(0, 2, "V")
            exp_s(1, 3)
            go_mm(1, 3)
            go_quant(0, 2, 2)
            go_mm(1, 0)
            exp_b(1, 2)
            go_quant(0, 0, 2)
            go_mm(1, 2)
            evac("v0", 0, "V")
            evac("v0", 1, "S")
            turn("v1", 0)
            make_w(1, 2, "G")
            go_copy(1, 0, "V")
            go_copy(1, 3, "S")
            turn("v1", 1)
            evac("v1", 0, "V")
            go_copy(1, 2, "S")
            go_mm(1, 1)
            shift(1, 3, "G")
            quant("v0", -1)
            evac("v1", 1, "S")
            shift(1, 0, "G")
            go_quant(1, 2, 2)
            go_copy(1, 1, "S")
            quant("v1", -1)
            ga_mm(0, 1)
            exp_b(1, 3)
            shift(1, 1, "G")
            go_quant(1, 0, 2)
            exp_b(1, 0)
            inv_z(1)
            make_w(1, 3, "G")
            ga_mm(1, 2)
            ga_sum(0, 1)
            ga_mm(0, 3)
            exp_b(1, 1)
            ga_mm(1, 0)
            ga_sum(1, 2)
            ga_mm(1, 1)
            recip_root(0, 1, 0, 512)
            ga_mm(0, 2)
            make_w(1, 0, "G")
            ga_w(0, 1)
            ga_mm(1, 3)
            ga_mm(0, 0)
            ga_sum(0, 3)
            make_w(1, 1, "G")
            ga_sum(1, 3)
            ga_w(0, 3)
            recip_root(0, 3, 0, 512)
            recip_sq(0, 1, 0, 512, "G")
            ga_sum(1, 0)
            recip_root(1, 0, 256, 256)
            recip_sq(0, 3, 0, 512, "S")
            ga_w(1, 3)
            recip_root(1, 2, 256, 256)
            final(0, 3, 0, 512, "G", 0)
            store(0, 0, 512, 3)
            ga_sum(1, 1)
            recip_root(1, 1, 256, 256)
            recip_sq(1, 0, 256, 256, "S")
            ga_sum(0, 0)
            recip_root(0, 0, 0, 512)
            final(0, 1, 0, 512, "G", 0)
            store(0, 0, 512, 1)
            ga_w(1, 2)
            recip_sq(1, 1, 256, 256, "S")
            recip_sq(1, 2, 256, 256, "S")
            ga_w(0, 0)
            recip_sq(0, 0, 0, 512, "S")
            final(1, 2, 256, 128, "G", 256)
            ga_w(1, 1)
            recip_root(1, 2, 0, 256)
            final(0, 0, 0, 512, "G", 0)
            store(0, 0, 512, 0)
            recip_root(1, 3, 256, 256)
            ga_sum(0, 2)
            recip_root(1, 3, 0, 256)
            ga_w(1, 0)
            recip_sq(1, 2, 0, 256, "S")
            recip_sq(1, 3, 256, 256, "S")
            final(1, 1, 256, 128, "G", 256)
            ga_w(0, 2)
            recip_sq(1, 3, 0, 256, "S")
            final(1, 2, 384, 128, "G", 256)
            recip_root(0, 2, 0, 512)
            final(1, 3, 0, 256, "V", 0)
            store(1, 0, 256, 3)
            final(1, 2, 0, 256, "V", 0)
            store(1, 0, 256, 2)
            recip_root(1, 0, 0, 256)
            final(1, 0, 384, 128, "V", 256)
            recip_sq(0, 2, 0, 512, "S")
            final(1, 1, 384, 128, "V", 256)
            final(1, 3, 384, 128, "V", 256)
            store(1, 384, 128, -1)
            final(1, 0, 256, 128, "V", 256)
            final(1, 3, 256, 128, "V", 256)
            store(1, 256, 128, -1)
            recip_root(1, 1, 0, 256)
            final(0, 2, 0, 512, "V", 0)
            store(0, 0, 512, 2)
            recip_sq(1, 0, 0, 256, "S")
            recip_sq(1, 1, 0, 256, "S")
            final(1, 0, 0, 256, "V", 0)
            store(1, 0, 256, 0)
            spread(1, 256, 128, "S")
            final(1, 1, 0, 256, "V", 0)
            store(1, 0, 256, 1)
            spread(0, 0, 512, "V")
            spread(1, 384, 128, "S")
            spread(1, 0, 256, "S")
            planes(1, 256, 128)
            planes(1, 384, 128)
            planes(0, 0, 512)
            planes(1, 0, 256)
